import numpy as np, ml_dtypes
CORES = [24,25,26,27,28,29,30,31]
N = 8
import mx_ref
BF = ml_dtypes.bfloat16
def gentries(a):
    return np.ascontiguousarray(a.reshape(8, 16, -1).transpose(0, 2, 1)).reshape(8, -1)
def gtable(e):
    e = np.asarray(e); return np.ascontiguousarray(e.reshape(8, -1, 16).transpose(0, 2, 1)).reshape(128, -1).astype(np.int32)
def gcols(t, e):
    v = np.concatenate([t.reshape(8, 16, -1, 4), np.zeros((8, 16, 1, 4), BF)], axis=2)
    return np.ascontiguousarray(np.stack([v[g][:, e[g]] for g in range(8)])).reshape(128, -1)
def tile(rs):
    return np.stack(rs, axis=2).reshape(128, -1).astype(BF)
def pick(q, e):
    c = np.concatenate([q[0].reshape(128, -1, 4), np.zeros((128, 1, 4), np.uint8)], axis=1); s = np.concatenate([q[1], np.ones((16, 1), np.uint8)], axis=1)
    return (np.ascontiguousarray(c[:, e].reshape(128, -1)), np.ascontiguousarray(s[:, e]))
def join(*qs):
    return (np.concatenate([q[0] for q in qs], axis=1), np.concatenate([q[1] for q in qs], axis=1))
def put(q, e, v):
    c, s = q[0].reshape(128, -1, 4).copy(), q[1].copy(); c[:, e] = v[0].reshape(128, -1, 4); s[:, e] = v[1]
    return (c.reshape(128, -1), s)
def pk(c, s):
    return (np.ascontiguousarray(c), mx_ref.live(s))
def emit(q):
    return q[0], q[1]
def packed(v, rng):
    q = [mx_ref.quantize(np.ascontiguousarray(v[r])) for r in range(N)]
    return np.stack([a for a, b in q]), np.stack([mx_ref.plane(b, rng) for a, b in q])
def values_of_codes():
    e, c = np.zeros((128, 128, 4), np.float32), np.zeros((128, 2, 4), np.uint8)
    e[np.arange(128), np.arange(128), 0] = 1
    c[:127, :, 0] = np.arange(256).reshape(2, 128).T[:127]
    return mx_ref.matmul(mx_ref.quantize(e.reshape(128, 512).astype(BF)), (c.reshape(128, 8), np.full((16, 2), 127, np.uint8))).T.reshape(-1).astype(np.float64)
CODE_VALUE, SCALE_VALUE = values_of_codes(), 2.0 ** (np.arange(256) - 127.0)
def decode(q):
    return (CODE_VALUE[q[0]].reshape(16, 8, -1, 4) * SCALE_VALUE[q[1]][:, None, :, None] + 0.0).reshape(128, -1).astype(np.float32)
def f(rng, *shape):
    return mx_ref.flush((rng.standard_normal(shape, dtype=np.float32) * np.exp2(rng.integers(-2, 3, shape[:-1] + (1,)))).astype(BF))
def wide(rng, *shape, cols=0):
    v = rng.standard_normal(shape, dtype=np.float32) * np.exp2(rng.integers(-12, 13, shape)).astype(np.float32)
    if cols: v *= np.repeat(np.exp2(rng.integers(-cols, cols + 1, shape[:-2] + (1, shape[-1] // 4))) * (rng.random(shape[:-2] + (1, shape[-1] // 4)) > 0.0625), 4, axis=-1).astype(np.float32)
    return mx_ref.flush(v.astype(BF))
C, H = 320, 160
STEP = [1, 2, 4]
def numbers_of(rng):
    return {"x": np.array(f(rng, N, 128, 4 * C)), "u": np.array(f(rng, N, 128, 512)), "v": np.array(f(rng, N, 128, 512))}
def lists(rng):
    e = np.tile(np.arange(C), (N, 8, 1))
    q = rng.permuted(e, axis=2)
    p = np.zeros((N, 8, C), np.int64)
    np.put_along_axis(p, q, np.ascontiguousarray(q.reshape(N, 8, H, 2)[..., ::-1]).reshape(N, 8, C), axis=2)
    return rng.permuted(e, axis=2), p
def stored(n, p):
    return {k: np.stack([gtable(e[r]) for r in range(N)]) for k, e in (("nx", n), ("iv", np.argsort(n, axis=2)), ("pr", p))}
def layer(rng, still=[]):
    w = np.array(f(rng, 128, 2048)).reshape(8, 16, 4, 8, 16, 4)
    for i in still:
        w[:, i] = 0
        w[:, :, :, :, i] = 0
    return w
def weights(rng, w):
    c, s = packed(np.stack([np.ascontiguousarray(w).reshape(128, 2048)] * N), rng)
    return {"wc": c, "ws": s}
def setup_inputs(rng):
    return {**numbers_of(rng), **stored(*lists(rng)), **weights(rng, layer(rng))}
def setup_inputs_ties(rng):
    d = numbers_of(rng)
    n, p = lists(rng)
    o = rng.permutation(N)
    k = rng.integers(-1, 2, (N, 8, C))
    k[o[1]] = 1
    k[o[2]] = 1
    t = rng.integers(0, 2, (8, C))
    t = np.where(np.arange(C) < p[o[3]], t, 1 - np.take_along_axis(t, p[o[3]], axis=1))
    k[o[3]] = np.where(t == 1, 1, rng.integers(-1, 1, (8, C)))
    a = np.exp2(rng.integers(-3, 4, (8, 1)).astype(np.float32))
    x = d["x"].reshape(N, 8, 16, C, 4)
    x[:, :, 0] = 0
    x[:, :, 0, :, 0] = k.astype(np.float32).astype(BF)
    x[:, :, 8:] = 0
    x[:, :, 8, :, 0] = (-1.125 * a).astype(BF)
    x[:, :, 10, :, 0] = (-0.0703125 * a).astype(BF)
    u = d["u"].reshape(N, 128, 128, 4)
    u[:, :, ::16] = 0
    for r in range(N):
        for h in range(0, 128, 16): u[r, h, h, 0] = 0.0 if r == o[0] else -1.0 if r == o[2] else 1.0
    w = layer(rng, [0])
    w[:, :, :, :, 8:] = 0
    for g in range(8):
        w[g, 8, 0, g, 8, 0] = -28.0
        for b in range(4): w[g, 10, b, g, 9, 0] = -2.0 ** (b - 5)
    return {"x": x.reshape(N, 128, 4 * C), "u": u.reshape(N, 128, 512), "v": d["v"], **stored(n, p), **weights(rng, w)}
def setup_inputs_near(rng):
    d = numbers_of(rng)
    k = np.where(rng.permutation(N) % 2 == 0, 2.0 ** -30, 1.0)
    x = rng.choice([-1.0, 1.0], (N, 8, 16, C, 4)) * (1.0 + 0.125 * rng.integers(0, 8, (N, 8, 16, C, 4))) * 64.0 * k[:, None, None, None, None]
    x[:, :, :9] = 0
    s = rng.integers(-1, 2, (N, 8, C)) * k[:, None, None]
    x[:, :, 0, :, 0] = 1.125 * s
    x[:, :, 1, :, 0] = -1.25 * s
    x[:, :, 7, :, 0] = k[:, None, None]
    x[:, :, 8, :, 0] = rng.choice([-1.0, 1.0], (N, 8, C)) * k[:, None, None]
    x[:, :, 9, :, 0] = 64.0 * k[:, None, None]
    for r in range(N):
        at = [0, C - 1, int(rng.integers(C)), int(rng.integers(C))]
        for g, j in zip(rng.permutation(8)[:4], at): x[r, g, 0, j, 0] = 2.0 ** 30 * rng.choice([-1.0, 1.0])
    u = d["u"].reshape(N, 128, 128, 4)
    u[:, :, ::16] = 0
    for h in range(0, 128, 16):
        u[:, h, h, 0] = (1.125 * k).astype(np.float32).astype(BF)
        u[:, h + 1, h, 0] = k.astype(np.float32).astype(BF)
        u[:, h + 2, h, 0] = k.astype(np.float32).astype(BF)
    w = layer(rng, list(range(10)))
    for g in range(8):
        w[g, 8, 0, g, 2, 0] = 2.0 ** -8
        w[g, 9, 0, g, 7, 0] = 1.0
    return {"x": x.astype(np.float32).reshape(N, 128, 4 * C).astype(BF), "u": u.reshape(N, 128, 512), "v": d["v"], **stored(*lists(rng)), **weights(rng, w)}
def setup_inputs_odd(rng):
    d = numbers_of(rng)
    x = (1.0 + (2 * rng.integers(0, 64, (N, 16, 8, C, 4)) + 1) * 2.0 ** -7) * np.exp2(-rng.integers(0, 7, (N, 16, 8, C, 4)).astype(np.float64)) * rng.choice([-1.0, 1.0], (N, 16, 8, C, 4))
    x[:, :, 0, :, 0] = rng.choice([1.96875, 1.875], (N, 16, C)) * 2.0 ** 8 * rng.choice([-1.0, 1.0], (N, 16, C))
    k = np.exp2(rng.integers(0, 4, (N, 8, C)) - 5.0)
    r = int(rng.integers(N))
    k[r] = k[r, :1].copy()
    x[:, ::2, 1, :, 0] = k * (1.0 + 0.125 * rng.integers(0, 2, (N, 8, C)))
    x[:, ::2, 2, :, 0] = k
    x[r, 0, 1, :, 0] = k[r, 0]
    u = d["u"].reshape(N, 16, 8, 128, 4)
    u[:, :, :, ::16] = 0
    for g in range(8):
        u[:, 2 * g, 1, 16 * g, 0] = 1.0
        u[:, 2 * g, 2, 16 * g, 0] = -1.0
    for g, i, e in ((0, 1, 4), (3, 2, 2)):
        u[r, :, :, 16 * g] = 0
        u[r, 0, i, 16 * g, 0] = 1.0
        u[r, 2 * e, 1, 16 * g, 0] = 1.875 * 2.0 ** -25
        u[r, 14, 2, 16 * g, 0] = -1.0
    return {"x": x.astype(np.float32).reshape(N, 128, 4 * C).astype(BF), "u": u.reshape(N, 128, 512), "v": d["v"], **stored(*lists(rng)), **weights(rng, layer(rng, [0, 1, 2, 8]))}
def setup_inputs_ends(rng):
    d = numbers_of(rng)
    o, e = rng.permutation(N) % 4, rng.permutation(N) % 4
    c = rng.choice([-1.0, 1.0], (N, C))
    c[:, H:] = -c[:, :H][:, ::-1]
    s = rng.choice([-1.0, 1.0], (N, 128, C, 4))
    s[o == 0] = -1
    s[o == 1] = c[o == 1][:, None, :, None]
    s[o == 3] = s[o == 3][:, :, :1]
    x = s * (0.63 + 0.06 * rng.random((N, 128, C, 4))) * 2.0 ** 30
    x[o == 3] = s[o == 3] * 2.0 ** -26
    x[o == 3, 48:64] = s[o == 3, 48:64] * 2.0 ** -30
    x[:, 120:] = s[:, 120:] * 2.0 ** -29
    a = np.stack([rng.permutation(8) % 2 * 2.0 - 1.0 for r in range(N)]) * np.where(o < 2, 2.0 ** 30, 2.0 ** -30)[:, None]
    u = d["u"].reshape(N, 128, 128, 4)
    u[:, :, ::16] = a.astype(np.float32).astype(BF)[:, None, :, None]
    v = rng.choice([-1.0, 1.0], (N, 128, 512)) * np.where(o % 2 == 0, 2.0 ** 30, 2.0 ** -30)[:, None, None]
    n, p = lists(rng)
    i = np.arange(C)
    p[o == 0] = i ^ 1
    p[o == 1] = C - 1 - i
    p[o == 2] = (i + H) % C
    n[e == 0] = i
    n[e == 1] = C - 1 - i
    n[e == 2] = (i + 1) % C
    n[e == 3] = p[e == 3]
    w = np.zeros((128, 4, 128, 4), np.float32)
    j = np.arange(128)
    for b in range(4): w[j, b, j, b] = np.where(j // 16 == 3, 0.0, np.where(j < 120, -4.0, 256.0))
    return {"x": x.astype(np.float32).reshape(N, 128, 4 * C).astype(BF), "u": u.reshape(N, 128, 512), "v": v.astype(np.float32).astype(BF), **stored(n, p), **weights(rng, w.astype(BF))}
def setup_inputs_spread(rng):
    d = setup_inputs(rng)
    d["x"] = wide(rng, N, 128, 4 * C, cols=6)
    return d
def check_inputs(d):
    b = []
    for k in ("x", "u", "v"):
        a = np.abs(d[k].astype(np.float32))
        if not (np.isfinite(a).all() and ((a == 0) | (a >= 2.0 ** -30) & (a <= 2.0 ** 30)).all()): b.append("a value of " + k)
    none, least, most = [emit(mx_ref.quantize(np.full((128, 16), k, np.float32).astype(BF)))[1][0, 0] for k in (0.0, 2.0 ** -8, 2.0 ** 8)]
    full = np.arange(C)
    for k in ("nx", "iv", "pr"):
        if not ((d[k] >= 0) & (d[k] < C)).all(): b.append("an entry of " + k)
    for r in range(N):
        n, i, p = [np.clip(gentries(d[k][r]), 0, C - 1) for k in ("nx", "iv", "pr")]
        if not (np.take_along_axis(i, n, axis=1) == full).all(): b.append("iv: not the inverse of nx")
        if not (np.take_along_axis(p, p, axis=1) == full).all() or (p == full).any(): b.append("pr: not pairs")
        if ((d["wc"][r] == 0x7F) | (d["wc"][r] == 0xFF)).any(): b.append("wc: a code that is no number")
        s = mx_ref.live(d["ws"][r])
        if ((s != none) & ((s < least) | (s > most))).any(): b.append("ws: a scale out of range")
        if (((d["wc"][r].reshape(16, 8, 512, 4) & 0x7F) != 0) & (s == none)[:, None, :, None]).any(): b.append("wc: a code other than zero under the scale of zeros")
        if (d["wc"][r] != d["wc"][0]).any() or (s != mx_ref.live(d["ws"][0])).any(): b.append("wc and ws: not the same on all ranks")
    return b
def reference(x, u, v, nx, iv, pr, wc, ws):
    qu = [mx_ref.quantize(u[r]) for r in range(N)]
    lay = [[pick(pk(wc[r], ws[r]), np.arange(128 * b, 128 * b + 128)) for b in range(4)] for r in range(N)]
    nxt, inv, pair = [[gentries(t[r]).astype(np.int64) for r in range(N)] for t in (nx, iv, pr)]
    now = [x[r] for r in range(N)]
    for step in STEP:
        had, made = [], []
        for r in range(N):
            n, m = nxt[r], inv[r]
            q = mx_ref.quantize(now[r])
            had.append(decode(q).astype(BF))
            bit = mx_ref.matmul(qu[r], q)[::16] > 0
            t = np.where(bit == np.take_along_axis(bit, pair[r], axis=1), pair[r], np.arange(C))
            for g in (0, 2, 4, 6, 1, 3, 5, 7):
                h = (g + 1) % 8
                w = n[g][t[g][m[g]]]
                n[g], m[g] = n[g][t[g]], t[g][m[g]]
                n[h], m[h] = n[h][w], w[m[h]]
            one = gcols(had[r], n).astype(np.float32)
            two = gcols(had[r], np.take_along_axis(n, n, axis=1)).astype(np.float32)
            z = mx_ref.quantize(((one + two) * np.float32(0.5)).astype(BF))
            made.append(mx_ref.quantize(tile([mx_ref.matmul(lay[r][b], z) * np.float32(0.03125) for b in range(4)])))
        for r in range(N):
            k = decode(join(pick(made[r], np.arange(H)), pick(made[r ^ step], np.arange(H, C)))).astype(BF)
            now[r] = (had[r].astype(np.float32) + gcols(k, inv[r]).astype(np.float32)).astype(BF)
    y, nl = np.zeros((N, 128, C), np.float32), np.zeros((N, 8, C), np.float32)
    oc, osc = np.zeros((N, 128, 4 * C), np.uint8), np.zeros((N, 16, C), np.uint8)
    for r in range(N):
        q = mx_ref.quantize(now[r])
        y[r] = mx_ref.matmul(mx_ref.quantize(v[r]), q)
        nl[r] = nxt[r]
        oc[r], osc[r] = emit(q)
    return {"y": y, "nl": nl, "oc": oc, "osc": osc}

@@ -1,0 +1,336 @@
+from concourse.mybir import dt, AluOpType, ActivationFunctionType
+import comms_topo
+
+C, HF = 320, 160
+ROUNDS = 3
+STEP = [1, 2, 4]
+BF, F32, I32, U16, U8, MXC = "bfloat16", "float32", "int32", "uint16", "uint8", "float8_e4m3fn_x4"
+
+
+def _scratch():
+    s = {}
+
+    def sb(dtype, **kw):
+        for k, n in kw.items():
+            s[k] = ("sbuf", [128, n], dtype)
+    sb(BF, xin=1280, xst=1280, zt=1280, ho=640, hp=640, ut=512, vt=512, et=516, fw=1280, gw=1280, g2=1280, xw=1280)
+    sb(BF, idr=C, mk=C, mke=C, rr=C, d0=C, thr=C, j16=C)
+    sb(BF, ner=C, ngr=C, p1=C, sge=C, sgg=C, spe=C, spg=C, s1=640, s2=640, nep=C, wer=C, b1=C, b2=C)
+    sb(BF, alm=C, ngm=C, as_=640, rw=C, nem=C, nes=C, tgr=C, wr=C, wr2=C, wt=C, mgm=C, mgs=C, mem=C, mes=C)
+    sb(F32, yo=C, nlf=C, nle=C, al=20, dd=40, ef=60, gf=60, t1=60, t2=60, mev=2, mod=2, pmf=2)
+    sb(F32, q1=40, qe=40, q2=40, qm=40, qt=40, fa=20, fb=20, fz=20, ha=20, hb=20, hc=20)
+    sb(I32, own=60, shd=60, upd=60, jp=C, pc=2, pa=2, pb=2, ai=20, ui=16)
+    sb(U16, lle=60, llg=60, ne=20, me=20, mg=20, te=20, tg=20, aL=20, sh=40, nL=20, mL=20, ul=16)
+    sb(MXC, tq=C, zq=C, hqo=HF, hqp=HF, uq=128, uu=256, vq=128, wq=512, eq0=128, eq1=128, eq2=128, eq3=128)
+    sb(U8, ts=C, zs=C, hso=HF, hsp=HF, us=128, uus=256, vs=128, wsp=512, es0=128, es1=128, es2=128, es3=128)
+    for k in range(ROUNDS):
+        s["lq%d" % k] = ("sbuf", [128, HF], MXC)
+        s["ls%d" % k] = ("sbuf", [128, HF], U8)
+    s["ps"] = ("psum", [128, 512 * 8], F32)
+    return s
+
+
+SCRATCH = _scratch()
+SEMAPHORES = ["qv", "qs", "qp", "qg"] + ["arr%d" % k for k in range(ROUNDS)] + ["loc%d" % k for k in range(ROUNDS)] + ["dm%d" % k for k in range(48)]
+
+
+def rank_program(g, core, T, topo):
+    rank = T.rank_of(core)
+    if rank is None:
+        return
+    A = AluOpType
+    CP, SG = ActivationFunctionType.Copy, ActivationFunctionType.Sign
+    V, S, P = g.vector, g.scalar, g.tensor
+    queue = {"v": V, "s": S, "p": P, "g": g, "y": g.sync}
+    semof = {"v": "qv", "s": "qs", "p": "qp", "g": "qg"}
+    cnt = {}
+    known = {q: {} for q in queue}
+    writer, readers, ndma = {}, {}, [0]
+
+    def need(q, tok):
+        if known[q].get(tok[1], 0) < tok[2]:
+            queue[q].wait_ge(T.sem[tok[1]], tok[2])
+            known[q][tok[1]] = tok[2]
+        for k, n in tok[3].items():
+            if known[q].get(k, 0) < n: known[q][k] = n
+
+    def order(q, who, reads, writes):
+        toks = []
+        for k in reads:
+            if k in writer: toks.append(writer[k])
+            if k[:2] == "ps": toks += [t for t in readers.get(k, []) if t[0] != who]
+        for k in writes:
+            if k in writer and writer[k][0] != who: toks.append(writer[k])
+            toks += [t for t in readers.get(k, []) if t[0] != who]
+        for t in sorted(toks, key=lambda t: -t[2]): need(q, t)
+
+    def note(tok, reads, writes):
+        for k in reads: readers.setdefault(k, []).append(tok)
+        for k in writes:
+            writer[k] = tok
+            readers[k] = []
+
+    def emit(q, fn, reads, writes):
+        order(q, q, reads, writes)
+        s = semof[q]
+        cnt[s] = cnt.get(s, 0) + 1
+        fn(queue[q]).then_inc(T.sem[s], 1)
+        note((q, s, cnt[s], dict(known[q])), reads, writes)
+
+    def dma(q, out, in_, reads, writes):
+        s = "dm%d" % ndma[0]
+        ndma[0] += 1
+        order(q, s, reads, writes)
+        queue[q].dma_start(out, in_).then_inc(T.sem[s], 16)
+        note((s, s, 16, dict(known[q])), reads, writes)
+
+    def vv(fn, r, w): emit("v", fn, r, w)
+    def gg(fn, r, w): emit("g", fn, r, w)
+    def tt(out, in0, in1, op, r, w): vv(lambda e: e.tensor_tensor(out, in0, in1, op), r, w)
+    def tsc(out, in0, s1, s2, ops, r, w): vv(lambda e: e.tensor_scalar(out, in0, s1, s2, *ops), r, w)
+    def cp(out, in_, r, w): vv(lambda e: e.tensor_copy(out, in_), r, w)
+    def act(out, in_, r, w, scale=1.0): emit("s", lambda e: e.activation(out, in_, CP) if scale == 1.0 else e.activation(out, in_, CP, scale=scale), r, w)
+    def quant(c, s, t, r, w): vv(lambda e: e.quantize_mx(c, s, t), r, w)
+    def scan(out, d, x, op, r, w): vv(lambda e: e.tensor_tensor_scan(out, d, x, 0.0, A.mult, op), r, w)
+
+    def mm(bank, n, a, sa, b, sb, r):
+        emit("p", lambda e: e.matmul_mx(T.ps[:, 512 * bank:512 * bank + n], a, sa, b, sb, True, True), r, ["ps%d" % bank])
+
+    def bank(i, n): return T.ps[:, 512 * i:512 * i + n]
+    def win(name, b): return T[name][:, C * b:C * b + C]
+    def row(name): return T[name][:]
+    def ends(name, lo=0, hi=C): return T[name][:, lo + 15:hi:16]
+
+    def comp(out, w, lst, lo=0, key=None):
+        act(row(out), row(w).indirect(T[lst][:, lo:lo + 20]), [w] + (key or [lst]), [out])
+
+    def compv(out, w, lst, lo=0):
+        cp(row(out), row(w).indirect(T[lst][:, lo:lo + 20]), [w, lst], [out])
+
+    def compm(out, w, lst, lo=0, key=None, mask="mk"):
+        tt(row(out), row(w).indirect(T[lst][:, lo:lo + 20]), row(mask), A.mult, [w, mask] + (key or [lst]), [out])
+
+    def sums(sc, x, lo=0): scan(T[sc][:, lo:lo + C], row("rr"), row(x), A.add, ["rr", x], [sc + "%d" % lo])
+    def tolist(l, sc): tsc(T[l][:], ends(sc), 160.0, None, [A.add], [sc + "0"], [l])
+
+    vv(lambda e: e.memset(T.shd[:], 0), [], ["shd"])
+    vv(lambda e: e.memset(T.upd[:], 0), [], ["upd"])
+    vv(lambda e: e.memset(T.et[:], 0.5), [], ["et"])
+    dma("y", T.ut[:], T.u[:], [], ["ut"])
+    dma("y", T.xin[:, 0:640], T.x[:, 0:640], [], ["xin0"])
+    lists = (T.pr, T.nx, T.iv)
+    for i, src in enumerate(lists): dma("s", T.own[:, 20 * i:20 * i + 20], src[:], [], ["own%d" % i])
+    for i, src in enumerate(lists): dma("s", T.shd[16:128, 20 * i:20 * i + 20], src[0:112, :], ["shd"], ["shd%d" % i])
+    for i, src in enumerate(lists): dma("s", T.upd[0:112, 20 * i:20 * i + 20], src[16:128, :], ["upd"], ["upd%d" % i])
+    dma("y", T.xin[:, 640:1280], T.x[:, 640:1280], [], ["xin1"])
+    dma("y", T.wq[:].bitcast(dt.uint8), T.wc[:], [], ["wq"])
+    dma("y", T.wsp[:], T.ws[:], [], ["wsp"])
+    dma("y", T.vt[:], T.v[:], [], ["vt"])
+
+    gg(lambda e: e.iota(T.pc[:, 0:1], [[0, 1]], 0, 1), [], ["pc"])
+    gg(lambda e: e.iota(T.ui[:], [[16, 2], [32, 4], [0, 2]], 0, 0), [], ["ui"])
+    gg(lambda e: e.iota(T.ai[:], [[16, 20]], 0, 0), [], ["ai"])
+    gg(lambda e: e.iota(T.jp[:], [[1, C]], 128, -1), [], ["jp"])
+    gg(lambda e: e.iota(T.idr[:], [[1, C]], -160, 0, allow_small_or_imprecise_dtypes=True), [], ["idr"])
+    gg(lambda e: e.affine_select(T.et[:], T.et[:], [[-1, 516]], A.is_equal, 0.0, 3, 4), ["et"], ["et"])
+    gg(lambda e: e.iota(T.j16[:], [[0, 20], [1, 16]], 0, 0, allow_small_or_imprecise_dtypes=True), [], ["j16"])
+    tsc(T.pa[:, 0:1], T.pc[:, 0:1], 15, None, [A.bitwise_and], ["pc"], ["pa"])
+    tsc(T.pb[:, 0:1], T.pc[:, 0:1], 31, None, [A.bitwise_and], ["pc"], ["pb"])
+    cp(T.ul[:], T.ui[:], ["ui"], ["ul"])
+    cp(T.pmf[:, 0:1], T.pa[:, 0:1], ["pa"], ["pmf"])
+    tsc(T.mev[:, 0:1], T.pb[:, 0:1], 16, None, [A.is_lt], ["pb"], ["mev"])
+    tsc(T.mod[:, 0:1], T.pb[:, 0:1], 16, None, [A.is_ge], ["pb"], ["mod"])
+    tsc(T.al[:], T.ai[:], T.pmf[:, 0:1], None, [A.add], ["ai", "pmf"], ["al"])
+    tsc(T.jp[:], T.jp[:], 15, None, [A.bitwise_and], ["jp"], ["jp"])
+    tsc(row("mk"), T.jp[:], 0, None, [A.is_equal], ["jp"], ["mk"])
+    tsc(row("d0"), row("mk"), -2.0, 2.0, [A.mult, A.add], ["mk"], ["d0"])
+    ow, sh, up = ["own0", "own1", "own2"], ["shd0", "shd1", "shd2"], ["upd0", "upd1", "upd2"]
+    tt(T.t1[:], T.own[:], T.shd[:], A.subtract, ow + sh, ["t1"])
+    tt(T.t2[:], T.upd[:], T.own[:], A.subtract, ow + up, ["t2"])
+    tsc(T.t1[:], T.t1[:], T.mev[:, 0:1], None, [A.mult], ["t1", "mev"], ["t1"])
+    tsc(T.t2[:], T.t2[:], T.mev[:, 0:1], None, [A.mult], ["t2", "mev"], ["t2"])
+    tt(T.ef[:], T.t1[:], T.shd[:], A.add, ["t1"] + sh, ["ef"])
+    tt(T.gf[:], T.t2[:], T.own[:], A.add, ["t2"] + ow, ["gf"])
+    cp(T.lle[:], T.ef[:], ["ef"], ["lle"])
+    cp(T.llg[:], T.gf[:], ["gf"], ["llg"])
+    comp("ner", "idr", "lle", 20)
+    quant(T.uq[:], T.us[:], T.ut[:], ["ut"], ["uq"])
+    cp(T.uu[:].bitcast(dt.uint32), T.uq[:].bitcast(dt.uint32).indirect(T.ul[:]), ["uq", "ul"], ["uu"])
+    act(T.uus[:], T.us[:].indirect(T.ul[:]), ["uq", "ul"], ["uus"])
+    for h in (0, 1): quant(T.tq[:, HF * h:HF * h + HF], T.ts[:, HF * h:HF * h + HF], T.xin[:, 640 * h:640 * h + 640], ["xin%d" % h], ["tq%d" % h])
+    scan(row("thr"), row("d0"), row("mk"), A.max, ["d0", "mk"], ["thr"])
+    for i, (f, l) in enumerate((("ef", "lle"), ("gf", "llg"))):
+        c = slice(20 * i, 20 * i + 20)
+        tt(T.dd[:, c], T[f][:, 0:20], T.al[:], A.subtract, [f, "al"], ["dd%d" % i])
+    comp("ngr", "idr", "llg", 20)
+
+    def unpackers():
+        for b in range(4):
+            quant(T["eq%d" % b][:], T["es%d" % b][:], T.et[:, 3 - b:515 - b], ["et"], ["eq%d" % b])
+
+    def layer(tile, h, b0):
+        c = slice(HF * h, HF * h + HF)
+        for b in range(4):
+            mm(b0 + b, HF, T.wq[:, 128 * b:128 * b + 128], T.wsp[:, 128 * b:128 * b + 128], T.zq[:, c], T.zs[:, c], ["wq", "wsp", "zq%d" % h])
+        for b in range(4):
+            act(T[tile][:, b:640:4], bank(b0 + b, HF), ["ps%d" % (b0 + b)], ["%s.%d" % (tile, b)], 0.03125)
+
+    def pack(tile, hq, hs): quant(T[hq][:], T[hs][:], T[tile][:], ["%s.%d" % (tile, b) for b in range(4)], [hq])
+
+    def unpack(hq, hs, h, b0):
+        for b in range(4):
+            mm(b0 + b, HF, T["eq%d" % b][:], T["es%d" % b][:], T[hq][:], T[hs][:], ["eq%d" % b, hq])
+        for b in range(4):
+            c = slice(C * b + HF * h, C * b + HF * h + HF)
+            tt(T.xw[:, c], T.gw[:, c], bank(b0 + b, HF), A.add, ["gw%d" % b, "ps%d" % (b0 + b)], ["xw%d.%d" % (b, h)])
+
+    def send(k, partner):
+        rid, pid, _ = topo.addr(partner)
+        m, n = topo.mask(core, partner), 2 * len(topo.engines(core, partner))
+        order("g", "remote", ["hqp"], [])
+        arr, loc = T.sem["arr%d" % k], T.sem["loc%d" % k]
+        g.remote_dma(T["lq%d" % k][:].bitcast(dt.uint8), T.hqp[:].bitcast(dt.uint8), arr, loc, pid, rid, m)
+        g.remote_dma(T["ls%d" % k][:], T.hsp[:], arr, loc, pid, rid, m)
+        note(("remote", "loc%d" % k, n, {}), ["hqp"], [])
+        note(("remote", "arr%d" % k, n, {}), [], ["lq%d" % k])
+        moved.append((k, n))
+
+    moved = []
+    for k in range(ROUNDS):
+        last = k == ROUNDS - 1
+        partner = T.cores[rank ^ STEP[k]]
+        mel, mgl, mlo = ("me", "mg", 0) if k else ("lle", "llg", 40)
+        ue, uf = (T.uu[:, 0:128], T.uus[:, 0:128]), (T.uu[:, 128:256], T.uus[:, 128:256])
+        for h in (0, 1): mm(4 + h, HF, *ue, T.tq[:, HF * h:HF * h + HF], T.ts[:, HF * h:HF * h + HF], ["uu", "uus", "tq%d" % h])
+        mm(6, C, *uf, T.tq[:], T.ts[:], ["uu", "uus", "tq0", "tq1"])
+        emit("s", lambda e: e.activation(T.sge[:, 0:HF], bank(4, HF), SG, bias=-(2.0 ** -93)), ["ps4"], ["sge0"])
+        tsc(T.sge[:, HF:C], bank(5, HF), 0.0, None, [A.is_gt], ["ps5"], ["sge1"])
+        act(row("spe"), row("sge").indirect(T.lle[:, 0:20]), ["sge0", "sge1", "lle"], ["spe"])
+
+        def turns(i, sg, sp, lst):
+            c, x = slice(20 * i, 20 * i + 20), "%d" % i
+            scan(T.s1[:, C * i:C * i + C], row("d0"), row(sg), A.max, ["d0"] + ([sg] if i else [sg + "0", sg + "1"]), ["s1" + x])
+            yield
+            tsc(T.q1[:, c], ends("s1", C * i, C * i + C), T.thr[:, 15:16], None, [A.is_ge], ["s1" + x, "thr"], ["q1" + x])
+            yield
+            scan(T.s2[:, C * i:C * i + C], row("d0"), row(sp), A.max, ["d0", sp], ["s2" + x])
+            yield
+            tsc(T.q2[:, c], ends("s2", C * i, C * i + C), T.thr[:, 15:16], None, [A.is_ge], ["s2" + x, "thr"], ["q2" + x])
+            yield
+            tt(T.qe[:, c], T.q2[:, c], T.q1[:, c], A.is_equal, ["q1" + x, "q2" + x], ["qe" + x])
+            yield
+            tt(T.qm[:, c], T.qe[:, c], T.dd[:, c], A.mult, ["qe" + x, "dd" + x], ["qm" + x])
+            yield
+            tt(T.qt[:, c], T.qm[:, c], T.al[:], A.add, ["qm" + x, "al"], ["qt" + x])
+            yield
+            cp(T[lst][:], T.qt[:, c], ["qt" + x], [lst])
+            yield
+        e, f = turns(0, "sge", "spe", "te"), turns(1, "sgg", "spg", "tg")
+        next(e)
+        tsc(row("sgg"), bank(6, C), 0.0, None, [A.is_gt], ["ps6"], ["sgg"])
+        comp("spg", "sgg", "llg")
+        if k == 0: unpackers()
+        for b in range(4):
+            mm(b, C, T["eq%d" % b][:], T["es%d" % b][:], T.tq[:], T.ts[:], ["eq%d" % b, "tq0", "tq1"])
+        if k == 0: comp("p1", "ngr", "lle", 20)
+        else: act(win("fw", 0), bank(0, C), ["ps0"], ["fw0"])
+        for w in "eefefefefefe": next(e if w == "e" else f)
+        comp("nep", "ner", "te")
+        comp("wer", "nep", mel, mlo)
+        for b in (1, 2, 3) if k else (0, 1, 2, 3): act(win("fw", b), bank(b, C), ["ps%d" % b], ["fw%d" % b])
+        if k == 0:
+            tsc(row("rr"), row("j16"), 0, None, [A.not_equal], ["j16"], ["rr"])
+            tsc(row("mke"), row("mk"), T.mev[:, 0:1], None, [A.mult], ["mk", "mev"], ["mke"])
+        compv("b1", "p1", "te")
+        next(f)
+        compv("b2", "b1", mel, mlo)
+        next(f)
+        next(f)
+        compm("alm", "wer", mgl, mlo)
+        compm("ngm", "b2", "tg")
+        sums("as_", "alm", 0)
+        sums("as_", "ngm", C)
+        for a in range(4):
+            c = 32 * ((a + 1) % 4)
+            tsc(T.sh[c:c + 32, :], T.as_[32 * a:32 * a + 32, 15:640:16], 160.0, None, [A.add], ["as_0", "as_%d" % C], ["sh%d" % a])
+        SH = ["sh%d" % a for a in range(4)]
+        comp("tgr", "idr", "tg")
+        comp("rw", "nep", "sh", 20, SH)
+        comp("ner", "rw", "sh", 0, SH)
+        comp("wr", "idr", "sh", 20, SH)
+        tsc(T.aL[:], ends("as_"), 160.0, None, [A.add], ["as_0"], ["aL"])
+        tsc(T.fz[:], ends("as_", C, 640), T.mod[:, 0:1], 160.0, [A.mult, A.add], ["as_%d" % C, "mod"], ["fz"])
+        compm("mgm", "tgr", "aL")
+        compm("nem", "rw", "sh", 0, SH, "mke")
+        sums("mgs", "mgm")
+        sums("nes", "nem")
+        tt(T.fb[:], ends("nes"), T.fz[:], A.add, ["nes0", "fz"], ["fb"])
+        cp(T.nL[:], T.fb[:], ["fb"], ["nL"])
+        if not last:
+            cp(T.ne[:], T.fb[:], ["fb"], ["ne"])
+            for a in range(4): dma("y", T.ne[32 * a + 16:32 * a + 32, :], T.nL[32 * a:32 * a + 16, :], ["nL", "ne"], ["ne%d" % a])
+        NE = ["ne"] + ["ne%d" % a for a in range(4)]
+        for b in (0, 2, 3): act(win("gw", b), win("fw", b).indirect(T.nL[:]), ["fw%d" % b, "nL"], ["gw%d" % b])
+        cp(win("gw", 1), win("fw", 1).indirect(T.nL[:]), ["fw1", "nL"], ["gw1"])
+        for h in (1, 0):
+            def copy(b):
+                c = slice(C * b + HF * h, C * b + HF * h + HF)
+                if h: cp(T.g2[:, c], T.gw[:, c], ["gw%d" % b], ["g2%d.%d" % (b, h)])
+                else: act(T.g2[:, c], T.gw[:, c], ["gw%d" % b], ["g2%d.%d" % (b, h)])
+
+            def mean(b):
+                c = slice(C * b + HF * h, C * b + HF * h + HF)
+                tt(T.zt[:, 640 * h + b:640 * h + 640:4], win("gw", b).indirect(T.nL[:, 10 * h:10 * h + 10]), T.g2[:, c], A.add, ["gw%d" % b, "g2%d.%d" % (b, h), "nL"], ["zt%d.%d" % (h, b)])
+            if h:
+                for fn, b in ((copy, 1), (copy, 0), (mean, 1), (mean, 0), (copy, 2), (mean, 2), (copy, 3), (mean, 3)): fn(b)
+            else:
+                for b in range(4): copy(b)
+                comp("wr2", "wr", "sh", 0, SH)
+                layer("hp", 1, 4)
+                for b in range(4): mean(b)
+                pack("hp", "hqp", "hsp")
+            c = slice(HF * h, HF * h + HF)
+            quant(T.zq[:, c], T.zs[:, c], T.zt[:, 640 * h:640 * h + 640], ["zt%d.%d" % (h, b) for b in range(4)], ["zq%d" % h])
+        send(k, partner)
+        comp("wt", "wr2", "te")
+        compm("mem", "wt", mel, mlo)
+        layer("ho", 0, 0)
+        sums("mes", "mem")
+        pack("ho", "hqo", "hso")
+        comp("ngr", "b2", "tg")
+        if not last: comp("p1", "ngr", "ne", 0, NE)
+        else:
+            for i, (o, r) in enumerate((("nle", "ner"), ("nlf", "ngr"))):
+                emit("s", lambda e: e.activation(row(o), row(r), ActivationFunctionType.Identity, bias=160.0), [r], [o])
+                dma("y", T.nl[i:8:2, :], T[o][0:128:32, :], [o], [])
+        tsc(T.ha[:], ends("mes"), T.mev[:, 0:1], 160.0, [A.mult, A.add], ["mes0", "mev"], ["ha"])
+        tsc(T.hb[:], ends("mgs"), T.mod[:, 0:1], None, [A.mult], ["mgs0", "mod"], ["hb"])
+        tt(T.hc[:], T.ha[:], T.hb[:], A.add, ["ha", "hb"], ["hc"])
+        unpack("hqo", "hso", 0, 4)
+        cp(T.mL[:], T.hc[:], ["hc"], ["mL"])
+        if not last:
+            tolist("mg", "mgs")
+            tolist("me", "mes")
+        unpack("lq%d" % k, "ls%d" % k, 1, 0)
+        def xs(b): return ["xw%d.0" % b, "xw%d.1" % b, "mL"]
+        for b in (0, 1): act(T.xst[:, b:1280:4], win("xw", b).indirect(T.mL[:]), xs(b), ["xst%d" % b], 2.0)
+        act(T.xst[:, 642:1280:4], win("xw", 2).indirect(T.mL[:, 10:20]), xs(2), ["xst2.1"], 2.0)
+        tsc(T.xst[:, 2:640:4], win("xw", 2).indirect(T.mL[:, 0:10]), 2.0, None, [A.mult], xs(2), ["xst2.0"])
+        tsc(T.xst[:, 3:1280:4], win("xw", 3).indirect(T.mL[:]), 2.0, None, [A.mult], xs(3), ["xst3"])
+        for h in (0, 1): quant(T.tq[:, HF * h:HF * h + HF], T.ts[:, HF * h:HF * h + HF], T.xst[:, 640 * h:640 * h + 640], ["xst0", "xst1", "xst2.%d" % h, "xst3"], ["tq%d" % h])
+        if k == 0: quant(T.vq[:], T.vs[:], T.vt[:], ["vt"], ["vq"])
+
+    for h in (0, 1):
+        c = slice(HF * h, HF * h + HF)
+        mm(6 + h, HF, T.vq[:], T.vs[:], T.tq[:, c], T.ts[:, c], ["vq", "tq%d" % h])
+    cp(T.yo[:, 0:HF], bank(6, HF), ["ps6"], ["yo0"])
+    act(T.yo[:, HF:C], bank(7, HF), ["ps7"], ["yo1"])
+    dma("y", T.oc[:], T.tq[:].bitcast(dt.uint8), ["tq0", "tq1"], [])
+    dma("y", T.y[:, 0:HF], T.yo[:, 0:HF], ["yo0"], [])
+    dma("s", T.y[:, HF:C], T.yo[:, HF:C], ["yo1"], [])
+    for i in range(4): dma("y" if i < 2 else "s", T.osc[4 * i:4 * i + 4, :], T.ts[32 * i:32 * i + 4, :], ["tq0", "tq1"], [])
+    for i in range(ndma[0]): need("g", ("x", "dm%d" % i, 16, {}))
+    for s, n in cnt.items(): need("g", ("x", s, n, {}))
+    for k, n in moved:
+        need("g", ("x", "loc%d" % k, n, {}))
+        need("g", ("x", "arr%d" % k, n, {}))

@@ -2,9 +2,10 @@ from concourse.mybir import dt, AluOpType, ActivationFunctionType
 import comms_topo
 
 C, HF = 320, 160
+T0 = 192
 ROUNDS = 3
 STEP = [1, 2, 4]
-BF, F32, I32, U16, U8, MXC = "bfloat16", "float32", "int32", "uint16", "uint8", "float8_e4m3fn_x4"
+BF, F32, F16, I32, U16, U8, MXC = "bfloat16", "float32", "float16", "int32", "uint16", "uint8", "float8_e4m3fn_x4"
 
 
 def _scratch():
@@ -13,14 +14,14 @@ def _scratch():
     def sb(dtype, **kw):
         for k, n in kw.items():
             s[k] = ("sbuf", [128, n], dtype)
-    sb(BF, xin=1280, xst=1280, zt=1280, ho=640, hp=640, ut=512, vt=512, et=516, fw=1280, gw=1280, g2=1280, xw=1280)
-    sb(BF, idr=C, mk=C, mke=C, rr=C, d0=C, thr=C, j16=C)
-    sb(BF, ner=C, ngr=C, p1=C, sge=C, sgg=C, spe=C, spg=C, s1=640, s2=640, nep=C, wer=C, b1=C, b2=C)
-    sb(BF, alm=C, ngm=C, as_=640, rw=C, nem=C, nes=C, tgr=C, wr=C, wr2=C, wt=C, mgm=C, mgs=C, mem=C, mes=C)
-    sb(F32, yo=C, nlf=C, nle=C, al=20, dd=40, ef=60, gf=60, t1=60, t2=60, mev=2, mod=2, pmf=2)
-    sb(F32, q1=40, qe=40, q2=40, qm=40, qt=40, fa=20, fb=20, fz=20, ha=20, hb=20, hc=20)
-    sb(I32, own=60, shd=60, upd=60, jp=C, pc=2, pa=2, pb=2, ai=20, ui=16)
-    sb(U16, lle=60, llg=60, ne=20, me=20, mg=20, te=20, tg=20, aL=20, sh=40, nL=20, mL=20, ul=16)
+    sb(BF, xin=1280, xst=1280, zt=1280, ho=640, hp=640, ut=512, vt=512, et=516)
+    sb(BF, fw=1280, f2=640, gw=640, g2=640, yw=640, xw=640, kw=640)
+    sb(BF, idr=C, dv=C, sa=C, sb_=C, sf=C, spf=C, c3=960, r3=960, fo=960, b2=C, w2=1280, nn=C, rr=C, mr=C)
+    sb(F16, q1=C, q2=C, sc=848, tr=48, sn=C, sm=C)
+    sb(F32, yo=C, nlf=C, i64=64, e0=64, e1=64, pm=2, pn=2, mev=2, mod=2, fix0=2, fix3=2)
+    sb(F32, t1=80, t2=80, bl=80, xb=60, qb=60, qo=60, dd=20)
+    sb(I32, lb=160, nx0=20, pc=2, pa=2, pb=2, ai=20, ui=16)
+    sb(U16, l1=20, me3=20, pe=20, pf=20, mf=20, l3=20, sh=40, nL=20, mL=20, ul=16)
     sb(MXC, tq=C, zq=C, hqo=HF, hqp=HF, uq=128, uu=256, vq=128, wq=512, eq0=128, eq1=128, eq2=128, eq3=128)
     sb(U8, ts=C, zs=C, hso=HF, hsp=HF, us=128, uus=256, vs=128, wsp=512, es0=128, es1=128, es2=128, es3=128)
     for k in range(ROUNDS):
@@ -31,7 +32,7 @@ def _scratch():
 
 
 SCRATCH = _scratch()
-SEMAPHORES = ["qv", "qs", "qp", "qg"] + ["arr%d" % k for k in range(ROUNDS)] + ["loc%d" % k for k in range(ROUNDS)] + ["dm%d" % k for k in range(48)]
+SEMAPHORES = ["qv", "qs", "qp", "qg"] + ["arr%d" % k for k in range(ROUNDS)] + ["loc%d" % k for k in range(ROUNDS)] + ["dm%d" % k for k in range(64)]
 
 
 def rank_program(g, core, T, topo):
@@ -60,7 +61,7 @@ def rank_program(g, core, T, topo):
             if k in writer: toks.append(writer[k])
             if k[:2] == "ps": toks += [t for t in readers.get(k, []) if t[0] != who]
         for k in writes:
-            if k in writer and writer[k][0] != who: toks.append(writer[k])
+            if k in writer and (writer[k][0] != who or who != "p"): toks.append(writer[k])
             toks += [t for t in readers.get(k, []) if t[0] != who]
         for t in sorted(toks, key=lambda t: -t[2]): need(q, t)
 
@@ -86,103 +87,135 @@ def rank_program(g, core, T, topo):
 
     def vv(fn, r, w): emit("v", fn, r, w)
     def gg(fn, r, w): emit("g", fn, r, w)
+    def fill(ap, c, w): vv(lambda e: e.memset(ap, c), [], w)
     def tt(out, in0, in1, op, r, w): vv(lambda e: e.tensor_tensor(out, in0, in1, op), r, w)
     def tsc(out, in0, s1, s2, ops, r, w): vv(lambda e: e.tensor_scalar(out, in0, s1, s2, *ops), r, w)
     def cp(out, in_, r, w): vv(lambda e: e.tensor_copy(out, in_), r, w)
     def act(out, in_, r, w, scale=1.0): emit("s", lambda e: e.activation(out, in_, CP) if scale == 1.0 else e.activation(out, in_, CP, scale=scale), r, w)
     def quant(c, s, t, r, w): vv(lambda e: e.quantize_mx(c, s, t), r, w)
-    def scan(out, d, x, op, r, w): vv(lambda e: e.tensor_tensor_scan(out, d, x, 0.0, A.mult, op), r, w)
+    def scan(out, d, x, ops, r, w): vv(lambda e: e.tensor_tensor_scan(out, d, x, 0.0, *ops), r, w)
+    def turn(out, in_, r, w): vv(lambda e: e.transpose(out, in_), r, w)
+    def count(out, pattern, base, w): gg(lambda e: e.iota(out, pattern, base, 0, allow_small_or_imprecise_dtypes=True), [], w)
+    def gcopy(out, in_, n, r, w): gg(lambda e: e.affine_select(out, in_, [[0, n]], A.is_ge, 0.0, 0, 0), r, w)
 
     def mm(bank, n, a, sa, b, sb, r):
         emit("p", lambda e: e.matmul_mx(T.ps[:, 512 * bank:512 * bank + n], a, sa, b, sb, True, True), r, ["ps%d" % bank])
 
     def bank(i, n): return T.ps[:, 512 * i:512 * i + n]
-    def win(name, b): return T[name][:, C * b:C * b + C]
     def row(name): return T[name][:]
-    def ends(name, lo=0, hi=C): return T[name][:, lo + 15:hi:16]
+    def ends(name): return T[name][:, 15:C:16]
+    def col(name): return T[name][:, 0:1]
+    def run(name, i, lo=0, hi=C): return T[name][:, C * i + lo:C * i + hi]
+    def two(name): return [name + "0", name + "1"]
+    def four(name): return [name + "%d" % a for a in range(4)]
+    DV = ["dv%d" % i for i in range(5)]
+    def pick(out, x, r): scan(T[out][:, 0:C], row("dv"), x, [A.add, A.min], DV + r, [out])
+    def tolist(out, sc): tsc(T[out][:], ends(sc), col("fix0"), 160.0, [A.add, A.add], [sc, "fix0"], [out])
+    CUT = ((0, T0), (T0, C))
+    def tquant(tile, h, r): quant(T.tq[:, CUT[h][0]:CUT[h][1]], T.ts[:, CUT[h][0]:CUT[h][1]], T[tile][:, 4 * CUT[h][0]:4 * CUT[h][1]], r, ["tq%d" % h])
 
-    def comp(out, w, lst, lo=0, key=None):
-        act(row(out), row(w).indirect(T[lst][:, lo:lo + 20]), [w] + (key or [lst]), [out])
+    def split(out, at, step, w, lst, lo, r, wr, cut=10):
+        cp(T[out][:, at:at + 16 * cut * step:step], w.indirect(T[lst][:, lo:lo + cut]), r, [wr + "0"])
+        act(T[out][:, at + 16 * cut * step:at + C * step:step], w.indirect(T[lst][:, lo + cut:lo + 20]), r, [wr + "1"])
 
-    def compv(out, w, lst, lo=0):
-        cp(row(out), row(w).indirect(T[lst][:, lo:lo + 20]), [w, lst], [out])
-
-    def compm(out, w, lst, lo=0, key=None, mask="mk"):
-        tt(row(out), row(w).indirect(T[lst][:, lo:lo + 20]), row(mask), A.mult, [w, mask] + (key or [lst]), [out])
-
-    def sums(sc, x, lo=0): scan(T[sc][:, lo:lo + C], row("rr"), row(x), A.add, ["rr", x], [sc + "%d" % lo])
-    def tolist(l, sc): tsc(T[l][:], ends(sc), 160.0, None, [A.add], [sc + "0"], [l])
-
-    vv(lambda e: e.memset(T.shd[:], 0), [], ["shd"])
-    vv(lambda e: e.memset(T.upd[:], 0), [], ["upd"])
-    vv(lambda e: e.memset(T.et[:], 0.5), [], ["et"])
+    fill(T.lb[:, 60:140], 0, ["lb3", "lb4", "lb5", "lb6"])
+    fill(T.et[:], 0.5, ["et"])
     dma("y", T.ut[:], T.u[:], [], ["ut"])
-    dma("y", T.xin[:, 0:640], T.x[:, 0:640], [], ["xin0"])
-    lists = (T.pr, T.nx, T.iv)
-    for i, src in enumerate(lists): dma("s", T.own[:, 20 * i:20 * i + 20], src[:], [], ["own%d" % i])
-    for i, src in enumerate(lists): dma("s", T.shd[16:128, 20 * i:20 * i + 20], src[0:112, :], ["shd"], ["shd%d" % i])
-    for i, src in enumerate(lists): dma("s", T.upd[0:112, 20 * i:20 * i + 20], src[16:128, :], ["upd"], ["upd%d" % i])
-    dma("y", T.xin[:, 640:1280], T.x[:, 640:1280], [], ["xin1"])
+    dma("s", T.nx0[:], T.nx[:], [], ["nx0"])
+    dma("y", T.xin[:, 0:4 * T0], T.x[:, 0:4 * T0], [], ["xin0"])
+    dma("s", T.lb[:, 40:60], T.pr[:], [], ["lb2"])
+    dma("y", T.xin[:, 4 * T0:1280], T.x[:, 4 * T0:1280], [], ["xin1"])
+    dma("s", T.lb[:, 20:40], T.iv[:], [], ["lb1"])
+    for i, src in enumerate((T.nx, T.iv, T.pr)): dma("sy"[i % 2], T.lb[16:128, 80 + 20 * i:100 + 20 * i], src[0:112, :], [], ["lb%d" % (4 + i)])
+    dma("y", T.lb[0:112, 60:80], T.iv[16:128, :], [], ["lb3"])
     dma("y", T.wq[:].bitcast(dt.uint8), T.wc[:], [], ["wq"])
     dma("y", T.wsp[:], T.ws[:], [], ["wsp"])
     dma("y", T.vt[:], T.v[:], [], ["vt"])
 
     gg(lambda e: e.iota(T.pc[:, 0:1], [[0, 1]], 0, 1), [], ["pc"])
-    gg(lambda e: e.iota(T.ui[:], [[16, 2], [32, 4], [0, 2]], 0, 0), [], ["ui"])
     gg(lambda e: e.iota(T.ai[:], [[16, 20]], 0, 0), [], ["ai"])
-    gg(lambda e: e.iota(T.jp[:], [[1, C]], 128, -1), [], ["jp"])
-    gg(lambda e: e.iota(T.idr[:], [[1, C]], -160, 0, allow_small_or_imprecise_dtypes=True), [], ["idr"])
+    count(T.i64[:], [[0, 4], [1, 16]], 0, ["i64"])
+    gg(lambda e: e.iota(T.ui[:], [[16, 2], [32, 4], [0, 2]], 0, 0), [], ["ui"])
+    count(row("idr"), [[1, C]], -160, ["idr"])
+    for out, n, f, w in ((T.c3[:, 0:960:3], C, 0.0, "c3a"), (T.c3[:, 1:960:3], C, 2.0, "c3b"), (T.qb[:, 0:60:3], 20, 0.0, "qb0"), (T.qb[:, 2:60:3], 20, 2.0, "qb2"), (T.xb[:, 0:60:3], 20, 0.0, "xb0")):
+        act(out, T.et[:, 0:n], ["et"], [w], f)
     gg(lambda e: e.affine_select(T.et[:], T.et[:], [[-1, 516]], A.is_equal, 0.0, 3, 4), ["et"], ["et"])
-    gg(lambda e: e.iota(T.j16[:], [[0, 20], [1, 16]], 0, 0, allow_small_or_imprecise_dtypes=True), [], ["j16"])
-    tsc(T.pa[:, 0:1], T.pc[:, 0:1], 15, None, [A.bitwise_and], ["pc"], ["pa"])
-    tsc(T.pb[:, 0:1], T.pc[:, 0:1], 31, None, [A.bitwise_and], ["pc"], ["pb"])
+    tsc(col("pa"), col("pc"), 15, None, [A.bitwise_and], ["pc"], ["pa"])
+    tsc(col("pb"), col("pc"), 31, None, [A.bitwise_and], ["pc"], ["pb"])
+    fill(T.sc[:, 335:527:16], 0.0, ["sc+"])
+    cp(col("pm"), col("pa"), ["pa"], ["pm"])
+    tsc(col("pn"), col("pa"), 1.0, None, [A.add], ["pa"], ["pn"])
+    tsc(col("mev"), col("pb"), 16, None, [A.is_lt], ["pb"], ["mev"])
+    tsc(col("mod"), col("pb"), 16, None, [A.is_ge], ["pb"], ["mod"])
+    for i in (0, 7): tsc(T.lb[:, 20 * i:20 * i + 20], T.ai[:], col("pm"), None, [A.add], ["ai", "pm"], ["lb%d" % i])
+    al = T.lb[:, 0:20]
+    tsc(T.e0[:], T.i64[:], col("pm"), 1024.0, [A.is_equal, A.mult], ["i64", "pm"], ["e0"])
+    tsc(T.e1[:], T.i64[:], col("pn"), -320.0, [A.is_equal, A.mult], ["i64", "pn"], ["e1"])
     cp(T.ul[:], T.ui[:], ["ui"], ["ul"])
-    cp(T.pmf[:, 0:1], T.pa[:, 0:1], ["pa"], ["pmf"])
-    tsc(T.mev[:, 0:1], T.pb[:, 0:1], 16, None, [A.is_lt], ["pb"], ["mev"])
-    tsc(T.mod[:, 0:1], T.pb[:, 0:1], 16, None, [A.is_ge], ["pb"], ["mod"])
-    tsc(T.al[:], T.ai[:], T.pmf[:, 0:1], None, [A.add], ["ai", "pmf"], ["al"])
-    tsc(T.jp[:], T.jp[:], 15, None, [A.bitwise_and], ["jp"], ["jp"])
-    tsc(row("mk"), T.jp[:], 0, None, [A.is_equal], ["jp"], ["mk"])
-    tsc(row("d0"), row("mk"), -2.0, 2.0, [A.mult, A.add], ["mk"], ["d0"])
-    ow, sh, up = ["own0", "own1", "own2"], ["shd0", "shd1", "shd2"], ["upd0", "upd1", "upd2"]
-    tt(T.t1[:], T.own[:], T.shd[:], A.subtract, ow + sh, ["t1"])
-    tt(T.t2[:], T.upd[:], T.own[:], A.subtract, ow + up, ["t2"])
-    tsc(T.t1[:], T.t1[:], T.mev[:, 0:1], None, [A.mult], ["t1", "mev"], ["t1"])
-    tsc(T.t2[:], T.t2[:], T.mev[:, 0:1], None, [A.mult], ["t2", "mev"], ["t2"])
-    tt(T.ef[:], T.t1[:], T.shd[:], A.add, ["t1"] + sh, ["ef"])
-    tt(T.gf[:], T.t2[:], T.own[:], A.add, ["t2"] + ow, ["gf"])
-    cp(T.lle[:], T.ef[:], ["ef"], ["lle"])
-    cp(T.llg[:], T.gf[:], ["gf"], ["llg"])
-    comp("ner", "idr", "lle", 20)
+    tsc(col("fix0"), col("pa"), 15, 320.0, [A.is_lt, A.mult], ["pa"], ["fix0"])
+    tt(T.dv[:, 0:64], T.e0[:], T.e1[:], A.add, ["e0", "e1"], ["dv0"])
+    for i in range(1, 5): act(T.dv[:, 64 * i:64 * i + 64], T.dv[:, 0:64], ["dv0"], ["dv%d" % i])
     quant(T.uq[:], T.us[:], T.ut[:], ["ut"], ["uq"])
-    cp(T.uu[:].bitcast(dt.uint32), T.uq[:].bitcast(dt.uint32).indirect(T.ul[:]), ["uq", "ul"], ["uu"])
-    act(T.uus[:], T.us[:].indirect(T.ul[:]), ["uq", "ul"], ["uus"])
-    for h in (0, 1): quant(T.tq[:, HF * h:HF * h + HF], T.ts[:, HF * h:HF * h + HF], T.xin[:, 640 * h:640 * h + 640], ["xin%d" % h], ["tq%d" % h])
-    scan(row("thr"), row("d0"), row("mk"), A.max, ["d0", "mk"], ["thr"])
-    for i, (f, l) in enumerate((("ef", "lle"), ("gf", "llg"))):
-        c = slice(20 * i, 20 * i + 20)
-        tt(T.dd[:, c], T[f][:, 0:20], T.al[:], A.subtract, [f, "al"], ["dd%d" % i])
-    comp("ngr", "idr", "llg", 20)
+    cp(T.nL[:], T.nx0[:], ["nx0"], ["nL"])
+    tsc(T.t1[:], T.lb[:, 0:80], col("mev"), None, [A.mult], ["lb0", "lb1", "lb2", "lb3", "mev"], ["t1"])
+    tsc(T.t2[:], T.lb[:, 80:160], col("mod"), None, [A.mult], ["lb4", "lb5", "lb6", "lb7", "mod"], ["t2"])
+    cp(T.uu[:, 0:128].bitcast(dt.uint32), T.uq[:].bitcast(dt.uint32).indirect(T.ul[:, 0:8]), ["uq", "ul"], ["uu0"])
+    act(T.uus[:, 0:128], T.us[:].indirect(T.ul[:, 0:8]), ["uq", "ul"], ["uus0"])
+    act(row("nn"), row("idr").indirect(T.nL[:]), ["idr", "nL"], two("nn"))
+    tt(T.bl[:], T.t1[:], T.t2[:], A.add, ["t1", "t2"], ["bl"])
+    tquant("xin", 0, ["xin0"])
+    cp(T.l1[:], T.bl[:, 0:20], ["bl"], ["l1"])
+    cp(T.pe[:], T.bl[:, 40:60], ["bl"], ["pe"])
+    tquant("xin", 1, ["xin1"])
+    cp(T.uu[:, 128:256].bitcast(dt.uint32), T.uq[:].bitcast(dt.uint32).indirect(T.ul[:, 8:16]), ["uq", "ul"], ["uu1"])
+    act(T.uus[:, 128:256], T.us[:].indirect(T.ul[:, 8:16]), ["uq", "ul"], ["uus1"])
 
-    def unpackers():
-        for b in range(4):
-            quant(T["eq%d" % b][:], T["es%d" % b][:], T.et[:, 3 - b:515 - b], ["et"], ["eq%d" % b])
+    def ahead_r(keys): act(row("rr"), row("nn").indirect(T.l1[:]), two("nn") + keys, ["rr"])
+    def ahead_rp(): act(T.r3[:, 0:960:3], row("rr").indirect(T.pe[:]), ["rr", "pe"], ["r3a"])
+    def ahead_neg(): tsc(T.r3[:, 1:960:3], row("rr"), -1.0, None, [A.mult], ["rr"], ["r3b"])
+    def ahead_pos(): gcopy(T.r3[:, 2:960:3], row("rr"), C, ["rr"], ["r3c"])
 
-    def layer(tile, h, b0):
+    def turn_tables():
+        tt(T.dd[:], T.lb[:, 40:60], al, A.subtract, ["lb2", "lb0"], ["dd"])
+        cp(T.xb[:, 2:60:3], T.bl[:, 60:80], ["bl"], ["xb2"])
+        tsc(T.me3[:], T.bl[:, 20:40], 3.0, 2.0, [A.mult, A.add], ["bl"], ["me3"])
+        tsc(T.xb[:, 1:60:3], T.dd[:], col("mod"), None, [A.mult], ["dd", "mod"], ["xb1"])
+
+    def shift_tables():
+        tsc(col("fix3"), col("fix0"), 3.0, 482.0, [A.mult, A.add], ["fix0"], ["fix3"])
+        fill(T.tr[:, 32:48], 0.0, ["tr+"])
+        fill(T.sh[:, 20:40], 0, ["sh+1"])
+        tsc(T.sh[:, 0:20], al, 960.0, None, [A.add], ["lb0"], ["sh+0"])
+
+    def unpackers(bs):
+        for b in bs: quant(T["eq%d" % b][:], T["es%d" % b][:], T.et[:, 3 - b:515 - b], ["et"], ["eq%d" % b])
+
+    def fmm(bs):
+        for b in bs: mm(b, C, T["eq%d" % b][:], T["es%d" % b][:], T.tq[:], T.ts[:], ["eq%d" % b, "tq0", "tq1"])
+
+    def fcopy(b):
+        act(run("fw", b), bank(b, C), ["ps%d" % b], ["fw%d" % b], 2.0 if b > 1 else 1.0)
+        if b > 1: dma("y", run("f2", b - 2), run("fw", b), ["fw%d" % b], ["f2%d" % b])
+
+    def layer(h, b0):
         c = slice(HF * h, HF * h + HF)
         for b in range(4):
             mm(b0 + b, HF, T.wq[:, 128 * b:128 * b + 128], T.wsp[:, 128 * b:128 * b + 128], T.zq[:, c], T.zs[:, c], ["wq", "wsp", "zq%d" % h])
+
+    def htile(tile, b0):
         for b in range(4):
             act(T[tile][:, b:640:4], bank(b0 + b, HF), ["ps%d" % (b0 + b)], ["%s.%d" % (tile, b)], 0.03125)
 
     def pack(tile, hq, hs): quant(T[hq][:], T[hs][:], T[tile][:], ["%s.%d" % (tile, b) for b in range(4)], [hq])
 
-    def unpack(hq, hs, h, b0):
-        for b in range(4):
+    def unpack(hq, hs, b0):
+        for b in (2, 0, 3, 1):
             mm(b0 + b, HF, T["eq%d" % b][:], T["es%d" % b][:], T[hq][:], T[hs][:], ["eq%d" % b, hq])
-        for b in range(4):
-            c = slice(C * b + HF * h, C * b + HF * h + HF)
-            tt(T.xw[:, c], T.gw[:, c], bank(b0 + b, HF), A.add, ["gw%d" % b, "ps%d" % (b0 + b)], ["xw%d.%d" % (b, h)])
+
+    def xsum(h, b0, b): tt(run("xw", b, HF * h, HF * h + HF), run("gw", b, HF * h, HF * h + HF), bank(b0 + b, HF), A.add, ["gw%d" % b, "ps%d" % (b0 + b)], ["xw%d.%d" % (b, h)])
+
+    def kcopy(h, b0):
+        for b in (2, 3): act(run("kw", b - 2, HF * h, HF * h + HF), bank(b0 + b, HF), ["ps%d" % (b0 + b)], ["kw%d.%d" % (b, h)], 2.0)
 
     def send(k, partner):
         rid, pid, _ = topo.addr(partner)
@@ -195,142 +228,169 @@ def rank_program(g, core, T, topo):
         note(("remote", "arr%d" % k, n, {}), [], ["lq%d" % k])
         moved.append((k, n))
 
+    def cross(out, src, up, r, w):
+        for a in range(4):
+            lo, hi = slice(32 * a, 32 * a + 16), slice(32 * a + 16, 32 * a + 32)
+            dma("y", T[out][lo if up else hi, :], T[src][hi if up else lo, :], r, ["%s%d" % (w, a)])
+
+    def products(h):
+        lo, hi = CUT[h]
+        for i in (0, 1): mm(4 + 2 * i + h, hi - lo, T.uu[:, 128 * i:128 * i + 128], T.uus[:, 128 * i:128 * i + 128], T.tq[:, lo:hi], T.ts[:, lo:hi], ["uu%d" % i, "uus%d" % i, "tq%d" % h])
+
+    def signs(on, name, h):
+        lo, hi = CUT[h]
+        b = 4 + 2 * (name == "sf") + h
+        if on == "v": tsc(T[name][:, lo:hi], bank(b, hi - lo), 0.0, None, [A.is_gt], ["ps%d" % b], [name + "%d" % h])
+        else: emit("s", lambda e: e.activation(T[name][:, lo:hi], bank(b, hi - lo), SG, bias=-(2.0 ** -93)), ["ps%d" % b], [name + "%d" % h])
+
+    def agree(h):
+        lo, hi = CUT[h]
+        tt(T.c3[:, 3 * lo + 2:3 * hi:3], row("sa").indirect(T.pe[:, lo // 16:hi // 16]), T.sb_[:, lo:hi], A.is_equal, two("sa") + ["sb_%d" % h, "pe"], ["c3c%d" % h])
+
+    def choose(h):
+        c = slice(3 * CUT[h][0], 3 * CUT[h][1])
+        scan(T.fo[:, c], T.c3[:, c], T.r3[:, c], [A.mult, A.add], ["c3a", "c3b", "c3c%d" % h, "r3a", "r3b", "r3c"], ["fo%d" % h])
+
     moved = []
+    products(0)
+    products(1)
+    ahead_r(["l1"])
+    cp(T.pf[:], T.lb[:, 40:60], ["lb2"], ["pf"])
+    signs("v", "sa", 0)
+    signs("v", "sb_", 0)
+    signs("v", "sa", 1)
+    signs("v", "sb_", 1)
+    ahead_pos()
+    count(T.w2[:, 0:960], [[0, 960]], 0, two("rw"))
+    signs("s", "sf", 0)
+    ahead_rp()
+    signs("s", "sf", 1)
+    turn_tables()
     for k in range(ROUNDS):
         last = k == ROUNDS - 1
         partner = T.cores[rank ^ STEP[k]]
-        mel, mgl, mlo = ("me", "mg", 0) if k else ("lle", "llg", 40)
-        ue, uf = (T.uu[:, 0:128], T.uus[:, 0:128]), (T.uu[:, 128:256], T.uus[:, 128:256])
-        for h in (0, 1): mm(4 + h, HF, *ue, T.tq[:, HF * h:HF * h + HF], T.ts[:, HF * h:HF * h + HF], ["uu", "uus", "tq%d" % h])
-        mm(6, C, *uf, T.tq[:], T.ts[:], ["uu", "uus", "tq0", "tq1"])
-        emit("s", lambda e: e.activation(T.sge[:, 0:HF], bank(4, HF), SG, bias=-(2.0 ** -93)), ["ps4"], ["sge0"])
-        tsc(T.sge[:, HF:C], bank(5, HF), 0.0, None, [A.is_gt], ["ps5"], ["sge1"])
-        act(row("spe"), row("sge").indirect(T.lle[:, 0:20]), ["sge0", "sge1", "lle"], ["spe"])
-
-        def turns(i, sg, sp, lst):
-            c, x = slice(20 * i, 20 * i + 20), "%d" % i
-            scan(T.s1[:, C * i:C * i + C], row("d0"), row(sg), A.max, ["d0"] + ([sg] if i else [sg + "0", sg + "1"]), ["s1" + x])
-            yield
-            tsc(T.q1[:, c], ends("s1", C * i, C * i + C), T.thr[:, 15:16], None, [A.is_ge], ["s1" + x, "thr"], ["q1" + x])
-            yield
-            scan(T.s2[:, C * i:C * i + C], row("d0"), row(sp), A.max, ["d0", sp], ["s2" + x])
-            yield
-            tsc(T.q2[:, c], ends("s2", C * i, C * i + C), T.thr[:, 15:16], None, [A.is_ge], ["s2" + x, "thr"], ["q2" + x])
-            yield
-            tt(T.qe[:, c], T.q2[:, c], T.q1[:, c], A.is_equal, ["q1" + x, "q2" + x], ["qe" + x])
-            yield
-            tt(T.qm[:, c], T.qe[:, c], T.dd[:, c], A.mult, ["qe" + x, "dd" + x], ["qm" + x])
-            yield
-            tt(T.qt[:, c], T.qm[:, c], T.al[:], A.add, ["qm" + x, "al"], ["qt" + x])
-            yield
-            cp(T[lst][:], T.qt[:, c], ["qt" + x], [lst])
-            yield
-        e, f = turns(0, "sge", "spe", "te"), turns(1, "sgg", "spg", "tg")
-        next(e)
-        tsc(row("sgg"), bank(6, C), 0.0, None, [A.is_gt], ["ps6"], ["sgg"])
-        comp("spg", "sgg", "llg")
-        if k == 0: unpackers()
-        for b in range(4):
-            mm(b, C, T["eq%d" % b][:], T["es%d" % b][:], T.tq[:], T.ts[:], ["eq%d" % b, "tq0", "tq1"])
-        if k == 0: comp("p1", "ngr", "lle", 20)
-        else: act(win("fw", 0), bank(0, C), ["ps0"], ["fw0"])
-        for w in "eefefefefefe": next(e if w == "e" else f)
-        comp("nep", "ner", "te")
-        comp("wer", "nep", mel, mlo)
-        for b in (1, 2, 3) if k else (0, 1, 2, 3): act(win("fw", b), bank(b, C), ["ps%d" % b], ["fw%d" % b])
+        act(row("spf"), row("sf").indirect(T.pf[:]), two("sf") + ["pf"], ["spf"])
+        if k: fmm((2, 3, 0, 1))
+        agree(0)
+        if k == 0: ahead_neg()
+        agree(1)
+        if k == 0: pick("q1", row("sf"), two("sf"))
+        choose(0)
+        pick("q2", row("spf"), ["spf"])
+        choose(1)
+        if k:
+            fcopy(2)
+        tt(T.qb[:, 1:60:3], ends("q1"), ends("q2"), A.is_equal, ["q1", "q2"], ["qb1"])
+        ME = ["me3"] + (four("me3") if k else [])
+        act(T.b2[:, 128:C], row("fo").indirect(T.me3[:, 8:20]), two("fo") + ME, ["b21"])
+        if k == 0: unpackers((2,))
+        scan(T.qo[:], T.xb[:], T.qb[:], [A.add, A.mult], ["xb0", "xb1", "xb2", "qb0", "qb1", "qb2"], ["qo"])
+        cp(T.b2[:, 0:128], row("fo").indirect(T.me3[:, 0:8]), two("fo") + ME, ["b20"])
+        cp(T.l3[:], T.qo[:, 2:60:3], ["qo"], ["l3"])
+        if k == 0: unpackers((3,))
+        split("w2", 960, 1, row("b2"), "l3", 0, two("b2") + ["l3"], "nm")
         if k == 0:
-            tsc(row("rr"), row("j16"), 0, None, [A.not_equal], ["j16"], ["rr"])
-            tsc(row("mke"), row("mk"), T.mev[:, 0:1], None, [A.mult], ["mk", "mev"], ["mke"])
-        compv("b1", "p1", "te")
-        next(f)
-        compv("b2", "b1", mel, mlo)
-        next(f)
-        next(f)
-        compm("alm", "wer", mgl, mlo)
-        compm("ngm", "b2", "tg")
-        sums("as_", "alm", 0)
-        sums("as_", "ngm", C)
+            shift_tables()
+            fmm((2, 3))
+            fcopy(2)
+        fcopy(3)
+        pick("sc", T.w2[:, 960:1280], two("nm"))
+        if k == 0: unpackers((0,))
+        turn(T.tr[:, 0:32], T.sc[:, 15:527:16], ["sc", "sc+"], ["tr"])
+        if k == 0: unpackers((1,))
+        turn(T.sc[:, 335:847:16], T.tr[:, 16:48], ["tr", "tr+"], ["sc+"])
+        if k == 0:
+            fmm((0, 1))
+            cp(T.mf[:], al, ["lb0"], ["mf"])
+        fcopy(0)
+        if k: fcopy(1)
         for a in range(4):
             c = 32 * ((a + 1) % 4)
-            tsc(T.sh[c:c + 32, :], T.as_[32 * a:32 * a + 32, 15:640:16], 160.0, None, [A.add], ["as_0", "as_%d" % C], ["sh%d" % a])
-        SH = ["sh%d" % a for a in range(4)]
-        comp("tgr", "idr", "tg")
-        comp("rw", "nep", "sh", 20, SH)
-        comp("ner", "rw", "sh", 0, SH)
-        comp("wr", "idr", "sh", 20, SH)
-        tsc(T.aL[:], ends("as_"), 160.0, None, [A.add], ["as_0"], ["aL"])
-        tsc(T.fz[:], ends("as_", C, 640), T.mod[:, 0:1], 160.0, [A.mult, A.add], ["as_%d" % C, "mod"], ["fz"])
-        compm("mgm", "tgr", "aL")
-        compm("nem", "rw", "sh", 0, SH, "mke")
-        sums("mgs", "mgm")
-        sums("nes", "nem")
-        tt(T.fb[:], ends("nes"), T.fz[:], A.add, ["nes0", "fz"], ["fb"])
-        cp(T.nL[:], T.fb[:], ["fb"], ["nL"])
-        if not last:
-            cp(T.ne[:], T.fb[:], ["fb"], ["ne"])
-            for a in range(4): dma("y", T.ne[32 * a + 16:32 * a + 32, :], T.nL[32 * a:32 * a + 16, :], ["nL", "ne"], ["ne%d" % a])
-        NE = ["ne"] + ["ne%d" % a for a in range(4)]
-        for b in (0, 2, 3): act(win("gw", b), win("fw", b).indirect(T.nL[:]), ["fw%d" % b, "nL"], ["gw%d" % b])
-        cp(win("gw", 1), win("fw", 1).indirect(T.nL[:]), ["fw1", "nL"], ["gw1"])
+            tsc(T.sh[c:c + 16, :], T.sc[32 * a:32 * a + 16, 15:655:16], 3.0, T.fix3[32 * a:32 * a + 16, 0:1], [A.mult, A.add], ["sc", "sc+", "fix3", "sh+0", "sh+1"], ["sh%d" % a])
+        SH = four("sh") + two("sh+")
+        split("w2", 2, 3, row("fo"), "sh", 20, two("fo") + SH, "rw")
+        split("nn", 0, 1, row("w2"), "sh", 0, two("rw") + two("nm") + SH, "nn")
+        if k == 0: fcopy(1)
+        pick("sn", row("nn"), two("nn"))
+        if k == 0: quant(T.vq[:], T.vs[:], T.vt[:], ["vt"], ["vq"])
+        tolist("nL", "sn")
+        if not last: cross("l1", "nL", False, ["nL"], "l1")
+        else:
+            emit("s", lambda e: e.activation(row("nlf"), row("nn"), ActivationFunctionType.Identity, bias=160.0), two("nn"), ["nlf"])
+            dma("y", T.nl[:], T.nlf[0:128:16, :], ["nlf"], [])
+        for b in (0, 1): act(run("gw", b), run("fw", b).indirect(T.nL[:]), ["fw%d" % b, "nL"], ["gw%d" % b])
+        for b in (2, 3): tt(run("yw", b - 2), run("fw", b).indirect(T.nL[:]), run("f2", b - 2), A.add, ["fw%d" % b, "f2%d" % b, "nL"], ["yw%d" % b])
+        for b in (0, 1): gcopy(run("g2", b, 0, HF), run("gw", b, 0, HF), HF, ["gw%d" % b], ["g2%d.0" % b])
         for h in (1, 0):
-            def copy(b):
-                c = slice(C * b + HF * h, C * b + HF * h + HF)
-                if h: cp(T.g2[:, c], T.gw[:, c], ["gw%d" % b], ["g2%d.%d" % (b, h)])
-                else: act(T.g2[:, c], T.gw[:, c], ["gw%d" % b], ["g2%d.%d" % (b, h)])
-
-            def mean(b):
-                c = slice(C * b + HF * h, C * b + HF * h + HF)
-                tt(T.zt[:, 640 * h + b:640 * h + 640:4], win("gw", b).indirect(T.nL[:, 10 * h:10 * h + 10]), T.g2[:, c], A.add, ["gw%d" % b, "g2%d.%d" % (b, h), "nL"], ["zt%d.%d" % (h, b)])
+            n = T.nL[:, 10 * h:10 * h + 10]
+            for b in (2, 3): act(T.zt[:, 640 * h + b:640 * h + 640:4], run("yw", b - 2).indirect(n), ["yw%d" % b, "nL"], ["zt%d.%d" % (h, b)], 0.5)
             if h:
-                for fn, b in ((copy, 1), (copy, 0), (mean, 1), (mean, 0), (copy, 2), (mean, 2), (copy, 3), (mean, 3)): fn(b)
-            else:
-                for b in range(4): copy(b)
-                comp("wr2", "wr", "sh", 0, SH)
-                layer("hp", 1, 4)
-                for b in range(4): mean(b)
-                pack("hp", "hqp", "hsp")
+                for b in (0, 1): cp(run("g2", b, HF), run("gw", b, HF), ["gw%d" % b], ["g2%d.1" % b])
+            for b in (0, 1): tt(T.zt[:, 640 * h + b:640 * h + 640:4], run("gw", b).indirect(n), run("g2", b, HF * h, HF * h + HF), A.add, ["gw%d" % b, "g2%d.%d" % (b, h), "nL"], ["zt%d.%d" % (h, b)])
             c = slice(HF * h, HF * h + HF)
             quant(T.zq[:, c], T.zs[:, c], T.zt[:, 640 * h:640 * h + 640], ["zt%d.%d" % (h, b) for b in range(4)], ["zq%d" % h])
+            layer(h, 4 * h)
+        def invert(lo, hi): cp(row("mr").indirect(T.nL[:, lo:hi]), T.idr[:, 16 * lo:16 * hi], ["idr", "nL"], ["mr"])
+        htile("hp", 4)
+        invert(0, 4)
+        pack("hp", "hqp", "hsp")
         send(k, partner)
-        comp("wt", "wr2", "te")
-        compm("mem", "wt", mel, mlo)
-        layer("ho", 0, 0)
-        sums("mes", "mem")
+        htile("ho", 0)
+        invert(4, 12)
         pack("ho", "hqo", "hso")
-        comp("ngr", "b2", "tg")
-        if not last: comp("p1", "ngr", "ne", 0, NE)
-        else:
-            for i, (o, r) in enumerate((("nle", "ner"), ("nlf", "ngr"))):
-                emit("s", lambda e: e.activation(row(o), row(r), ActivationFunctionType.Identity, bias=160.0), [r], [o])
-                dma("y", T.nl[i:8:2, :], T[o][0:128:32, :], [o], [])
-        tsc(T.ha[:], ends("mes"), T.mev[:, 0:1], 160.0, [A.mult, A.add], ["mes0", "mev"], ["ha"])
-        tsc(T.hb[:], ends("mgs"), T.mod[:, 0:1], None, [A.mult], ["mgs0", "mod"], ["hb"])
-        tt(T.hc[:], T.ha[:], T.hb[:], A.add, ["ha", "hb"], ["hc"])
-        unpack("hqo", "hso", 0, 4)
-        cp(T.mL[:], T.hc[:], ["hc"], ["mL"])
+        unpack("hqo", "hso", 4)
+        invert(12, 20)
         if not last:
-            tolist("mg", "mgs")
-            tolist("me", "mes")
-        unpack("lq%d" % k, "ls%d" % k, 1, 0)
-        def xs(b): return ["xw%d.0" % b, "xw%d.1" % b, "mL"]
-        for b in (0, 1): act(T.xst[:, b:1280:4], win("xw", b).indirect(T.mL[:]), xs(b), ["xst%d" % b], 2.0)
-        act(T.xst[:, 642:1280:4], win("xw", 2).indirect(T.mL[:, 10:20]), xs(2), ["xst2.1"], 2.0)
-        tsc(T.xst[:, 2:640:4], win("xw", 2).indirect(T.mL[:, 0:10]), 2.0, None, [A.mult], xs(2), ["xst2.0"])
-        tsc(T.xst[:, 3:1280:4], win("xw", 3).indirect(T.mL[:]), 2.0, None, [A.mult], xs(3), ["xst3"])
-        for h in (0, 1): quant(T.tq[:, HF * h:HF * h + HF], T.ts[:, HF * h:HF * h + HF], T.xst[:, 640 * h:640 * h + 640], ["xst0", "xst1", "xst2.%d" % h, "xst3"], ["tq%d" % h])
-        if k == 0: quant(T.vq[:], T.vs[:], T.vt[:], ["vt"], ["vq"])
+            ahead_r(["l1"] + four("l1"))
+            ahead_pos()
+        unpack("lq%d" % k, "ls%d" % k, 0)
+        kcopy(0, 4)
+        xsum(0, 4, 0)
+        pick("sm", row("mr"), ["mr"])
+        xsum(0, 4, 1)
+        tolist("mL", "sm")
+        kcopy(1, 0)
+        xsum(1, 0, 0)
+        if not last:
+            tsc(T.me3[:], ends("sm"), 3.0, col("fix3"), [A.mult, A.add], ["sm", "fix3"], ["me3"] + four("me3"))
+            cross("me3", "me3", False, ["me3"], "me3")
+            cross("mf", "mL", True, ["mL", "mf"], "mf")
+        xsum(1, 0, 1)
+
+        def state(b, h):
+            lo, hi = CUT[h]
+            out, m, w = T.xst[:, 4 * lo + b:4 * hi:4], T.mL[:, lo // 16:hi // 16], ["xst%d.%d" % (h, b)]
+            if b < 2: act(out, run("xw", b).indirect(m), ["xw%d.0" % b, "xw%d.1" % b, "mL"], w, 2.0)
+            else: tt(out, run("kw", b - 2).indirect(m), run("fw", b, lo, hi), A.add, ["kw%d.0" % b, "kw%d.1" % b, "fw%d" % b, "mL"], w)
+
+        def squant(h): tquant("xst", h, ["xst%d.%d" % (h, b) for b in range(4)])
+        for b, h in ((0, 0), (1, 0), (0, 1), (1, 1), (2, 0), (3, 0), (2, 1)): state(b, h)
+        squant(0)
+        if not last:
+            products(0)
+            ahead_rp()
+        state(3, 1)
+        squant(1)
+        if not last:
+            products(1)
+            signs("v", "sf", 0)
+            ahead_neg()
+            for name, h in (("sa", 0), ("sb_", 0), ("sa", 1), ("sb_", 1)): signs("s", name, h)
+            signs("v", "sf", 1)
+            cp(T.xb[:, 2:60:3], T.mf[:], four("mf"), ["xb2"])
+            pick("q1", row("sf"), two("sf"))
 
     for h in (0, 1):
-        c = slice(HF * h, HF * h + HF)
-        mm(6 + h, HF, T.vq[:], T.vs[:], T.tq[:, c], T.ts[:, c], ["vq", "tq%d" % h])
-    cp(T.yo[:, 0:HF], bank(6, HF), ["ps6"], ["yo0"])
-    act(T.yo[:, HF:C], bank(7, HF), ["ps7"], ["yo1"])
-    dma("y", T.oc[:], T.tq[:].bitcast(dt.uint8), ["tq0", "tq1"], [])
-    dma("y", T.y[:, 0:HF], T.yo[:, 0:HF], ["yo0"], [])
-    dma("s", T.y[:, HF:C], T.yo[:, HF:C], ["yo1"], [])
+        lo, hi = CUT[h]
+        mm(6 + h, hi - lo, T.vq[:], T.vs[:], T.tq[:, lo:hi], T.ts[:, lo:hi], ["vq", "tq%d" % h])
+        dma("y", T.oc[:, 4 * lo:4 * hi], T.tq[:, lo:hi].bitcast(dt.uint8), ["tq%d" % h], [])
+    act(T.yo[:, 0:T0], bank(6, T0), ["ps6"], ["yo0"])
+    cp(T.yo[:, T0:C], bank(7, C - T0), ["ps7"], ["yo1"])
+    dma("s", T.y[:, 0:T0], T.yo[:, 0:T0], ["yo0"], [])
     for i in range(4): dma("y" if i < 2 else "s", T.osc[4 * i:4 * i + 4, :], T.ts[32 * i:32 * i + 4, :], ["tq0", "tq1"], [])
-    for i in range(ndma[0]): need("g", ("x", "dm%d" % i, 16, {}))
-    for s, n in cnt.items(): need("g", ("x", s, n, {}))
+    dma("y", T.y[:, T0:C], T.yo[:, T0:C], ["yo1"], [])
     for k, n in moved:
         need("g", ("x", "loc%d" % k, n, {}))
-        need("g", ("x", "arr%d" % k, n, {}))
+    for q, s in semof.items(): need("g", ("x", s, cnt[s], known[q]))
+    for i in range(ndma[0]):
+        if not any(known[q].get("dm%d" % i) for q in queue): need("g", ("x", "dm%d" % i, 16, {}))

@@ -5,7 +5,7 @@ C, HF = 320, 160
 T0 = 192
 ROUNDS = 3
 STEP = [1, 2, 4]
-BF, F32, F16, I32, U16, U8, MXC = "bfloat16", "float32", "float16", "int32", "uint16", "uint8", "float8_e4m3fn_x4"
+BF, F32, I32, U16, U8, MXC = "bfloat16", "float32", "int32", "uint16", "uint8", "float8_e4m3fn_x4"
 
 
 def _scratch():
@@ -16,12 +16,12 @@ def _scratch():
             s[k] = ("sbuf", [128, n], dtype)
     sb(BF, xin=1280, xst=1280, zt=1280, ho=640, hp=640, ut=512, vt=512, et=516)
     sb(BF, fw=1280, f2=640, gw=640, g2=640, yw=640, xw=640, kw=640)
-    sb(BF, idr=C, dv=C, sa=C, sb_=C, sf=C, spf=C, c3=960, r3=960, fo=960, b2=C, w2=1280, nn=C, rr=C, mr=C)
-    sb(F16, q1=C, q2=C, sc=848, tr=48, sn=C, sm=C)
-    sb(F32, yo=C, nlf=C, i64=64, e0=64, e1=64, pm=2, pn=2, mev=2, mod=2, fix0=2, fix3=2)
-    sb(F32, t1=80, t2=80, bl=80, xb=60, qb=60, qo=60, dd=20)
-    sb(I32, lb=160, nx0=20, pc=2, pa=2, pb=2, ai=20, ui=16)
-    sb(U16, l1=20, me3=20, pe=20, pf=20, mf=20, l3=20, sh=40, nL=20, mL=20, ul=16)
+    sb(BF, dv=C, sa=C, sb_=C, sf=C, spf=C, c3=960, r3=960, fo=960, b2=C, w2=960, tb=640, nn=C, rr=C, mr=640, ur=C)
+    sb(BF, q5=1632, sn=C, sm=C, su=C)
+    sb(F32, yo=C, nlf=C, i80=80, e0=64, e1=64, pm=2, mev=2, wd=2, we=2, mod=2, inv=2, sq=2, ua=2, ub=2)
+    sb(F32, t1=80, t2=80, bl=80, xb=100, qo=100, mF=20, mG=20)
+    sb(I32, lb=180, pc=2, pa=2, pb=2, ai=20, aj=40, ui=16)
+    sb(U16, lp=40, nf=40, me3=20, l4=20, l3=20, sh=40, mL=20, ul=16)
     sb(MXC, tq=C, zq=C, hqo=HF, hqp=HF, uq=128, uu=256, vq=128, wq=512, eq0=128, eq1=128, eq2=128, eq3=128)
     sb(U8, ts=C, zs=C, hso=HF, hsp=HF, us=128, uus=256, vs=128, wsp=512, es0=128, es1=128, es2=128, es3=128)
     for k in range(ROUNDS):
@@ -40,7 +40,7 @@ def rank_program(g, core, T, topo):
     if rank is None:
         return
     A = AluOpType
-    CP, SG = ActivationFunctionType.Copy, ActivationFunctionType.Sign
+    CP, ID, SG = ActivationFunctionType.Copy, ActivationFunctionType.Identity, ActivationFunctionType.Sign
     V, S, P = g.vector, g.scalar, g.tensor
     queue = {"v": V, "s": S, "p": P, "g": g, "y": g.sync}
     semof = {"v": "qv", "s": "qs", "p": "qp", "g": "qg"}
@@ -92,8 +92,9 @@ def rank_program(g, core, T, topo):
     def tsc(out, in0, s1, s2, ops, r, w): vv(lambda e: e.tensor_scalar(out, in0, s1, s2, *ops), r, w)
     def cp(out, in_, r, w): vv(lambda e: e.tensor_copy(out, in_), r, w)
     def act(out, in_, r, w, scale=1.0): emit("s", lambda e: e.activation(out, in_, CP) if scale == 1.0 else e.activation(out, in_, CP, scale=scale), r, w)
+    def affine(out, in_, scale, bias, r, w): emit("s", lambda e: e.activation(out, in_, ID, bias=bias, scale=scale), r, w)
     def quant(c, s, t, r, w): vv(lambda e: e.quantize_mx(c, s, t), r, w)
-    def scan(out, d, x, ops, r, w): vv(lambda e: e.tensor_tensor_scan(out, d, x, 0.0, *ops), r, w)
+    def scan(out, d, x, r, w): vv(lambda e: e.tensor_tensor_scan(out, d, x, 0.0, A.mult, A.add), r, w)
     def turn(out, in_, r, w): vv(lambda e: e.transpose(out, in_), r, w)
     def count(out, pattern, base, w): gg(lambda e: e.iota(out, pattern, base, 0, allow_small_or_imprecise_dtypes=True), [], w)
     def gcopy(out, in_, n, r, w): gg(lambda e: e.affine_select(out, in_, [[0, n]], A.is_ge, 0.0, 0, 0), r, w)
@@ -108,84 +109,80 @@ def rank_program(g, core, T, topo):
     def run(name, i, lo=0, hi=C): return T[name][:, C * i + lo:C * i + hi]
     def two(name): return [name + "0", name + "1"]
     def four(name): return [name + "%d" % a for a in range(4)]
+    def nL(a=0, b=20): return T.nf[:, a:b]
     DV = ["dv%d" % i for i in range(5)]
-    def pick(out, x, r): scan(T[out][:, 0:C], row("dv"), x, [A.add, A.min], DV + r, [out])
-    def tolist(out, sc): tsc(T[out][:], ends(sc), col("fix0"), 160.0, [A.add, A.add], [sc, "fix0"], [out])
+    def pick(out, x, r): scan(row(out), row("dv"), run(x, 0), DV + r, [out])
+    def tolist(out, sc, w): tsc(out, ends(sc), col("inv"), 160.25, [A.mult, A.add], [sc, "inv"], [w])
     CUT = ((0, T0), (T0, C))
     def tquant(tile, h, r): quant(T.tq[:, CUT[h][0]:CUT[h][1]], T.ts[:, CUT[h][0]:CUT[h][1]], T[tile][:, 4 * CUT[h][0]:4 * CUT[h][1]], r, ["tq%d" % h])
 
-    def split(out, at, step, w, lst, lo, r, wr, cut=10):
-        cp(T[out][:, at:at + 16 * cut * step:step], w.indirect(T[lst][:, lo:lo + cut]), r, [wr + "0"])
-        act(T[out][:, at + 16 * cut * step:at + C * step:step], w.indirect(T[lst][:, lo + cut:lo + 20]), r, [wr + "1"])
+    def part(on, out, at, w, lst, lo, a, b, r, wr):
+        (cp if on == "v" else act)(T[out][:, at + 16 * a:at + 16 * b], w.indirect(T[lst][:, lo + a:lo + b]), r, [wr])
 
-    fill(T.lb[:, 60:140], 0, ["lb3", "lb4", "lb5", "lb6"])
+    def split(out, at, w, lst, lo, r, wr, cut=10):
+        part("v", out, at, w, lst, lo, 0, cut, r, wr + "0")
+        part("s", out, at, w, lst, lo, cut, 20, r, wr + "1")
+
+    fill(T.lb[:, 80:160], 0, ["lb4", "lb5", "lb6", "lb7"])
     fill(T.et[:], 0.5, ["et"])
     dma("y", T.ut[:], T.u[:], [], ["ut"])
-    dma("s", T.nx0[:], T.nx[:], [], ["nx0"])
+    dma("s", T.lb[:, 0:20], T.nx[:], [], ["lb0"])
     dma("y", T.xin[:, 0:4 * T0], T.x[:, 0:4 * T0], [], ["xin0"])
-    dma("s", T.lb[:, 40:60], T.pr[:], [], ["lb2"])
+    dma("s", T.lb[:, 20:40], T.pr[:], [], ["lb1"])
     dma("y", T.xin[:, 4 * T0:1280], T.x[:, 4 * T0:1280], [], ["xin1"])
-    dma("s", T.lb[:, 20:40], T.iv[:], [], ["lb1"])
-    for i, src in enumerate((T.nx, T.iv, T.pr)): dma("sy"[i % 2], T.lb[16:128, 80 + 20 * i:100 + 20 * i], src[0:112, :], [], ["lb%d" % (4 + i)])
-    dma("y", T.lb[0:112, 60:80], T.iv[16:128, :], [], ["lb3"])
+    dma("s", T.lb[:, 60:80], T.iv[:], [], ["lb3"])
+    for i, src in enumerate((T.pr, T.nx, T.iv)): dma("sy"[i % 2], T.lb[16:128, 100 + 20 * i:120 + 20 * i], src[0:112, :], [], ["lb%d" % (5 + i)])
+    dma("y", T.lb[0:112, 80:100], T.iv[16:128, :], [], ["lb4"])
     dma("y", T.wq[:].bitcast(dt.uint8), T.wc[:], [], ["wq"])
     dma("y", T.wsp[:], T.ws[:], [], ["wsp"])
     dma("y", T.vt[:], T.v[:], [], ["vt"])
 
+    idr, al = T.w2[:, 640:960], T.lb[:, 40:60]
     gg(lambda e: e.iota(T.pc[:, 0:1], [[0, 1]], 0, 1), [], ["pc"])
-    gg(lambda e: e.iota(T.ai[:], [[16, 20]], 0, 0), [], ["ai"])
-    count(T.i64[:], [[0, 4], [1, 16]], 0, ["i64"])
     gg(lambda e: e.iota(T.ui[:], [[16, 2], [32, 4], [0, 2]], 0, 0), [], ["ui"])
-    count(row("idr"), [[1, C]], -160, ["idr"])
-    for out, n, f, w in ((T.c3[:, 0:960:3], C, 0.0, "c3a"), (T.c3[:, 1:960:3], C, 2.0, "c3b"), (T.qb[:, 0:60:3], 20, 0.0, "qb0"), (T.qb[:, 2:60:3], 20, 2.0, "qb2"), (T.xb[:, 0:60:3], 20, 0.0, "xb0")):
-        act(out, T.et[:, 0:n], ["et"], [w], f)
+    count(T.i80[:], [[0, 5], [1, 16]], 0, ["i80"])
+    gg(lambda e: e.iota(T.ai[:], [[16, 20]], 0, 0), [], ["ai"])
+    count(idr, [[1, C]], -160, ["idr"])
+    for out, f, w in ((T.c3[:, 0:960:3], 0.0, "c3a"), (T.c3[:, 1:960:3], -2.0, "c3b")): act(out, T.et[:, 0:C], ["et"], [w], f)
     gg(lambda e: e.affine_select(T.et[:], T.et[:], [[-1, 516]], A.is_equal, 0.0, 3, 4), ["et"], ["et"])
-    tsc(col("pa"), col("pc"), 15, None, [A.bitwise_and], ["pc"], ["pa"])
+    for out, v, w in ((T.q5[:, 43:1632:80], 0, "q5a"), (T.q5[:, 59:1632:80], 1, "q5b"), (T.q5[:, 107:1632:80], 1, "q5e"), (T.xb[:, 2:100:5], 0, "xb2")): count(out, [[0, 20]], v, [w])
     tsc(col("pb"), col("pc"), 31, None, [A.bitwise_and], ["pc"], ["pb"])
-    fill(T.sc[:, 335:527:16], 0.0, ["sc+"])
-    cp(col("pm"), col("pa"), ["pa"], ["pm"])
-    tsc(col("pn"), col("pa"), 1.0, None, [A.add], ["pa"], ["pn"])
-    tsc(col("mev"), col("pb"), 16, None, [A.is_lt], ["pb"], ["mev"])
-    tsc(col("mod"), col("pb"), 16, None, [A.is_ge], ["pb"], ["mod"])
-    for i in (0, 7): tsc(T.lb[:, 20 * i:20 * i + 20], T.ai[:], col("pm"), None, [A.add], ["ai", "pm"], ["lb%d" % i])
-    al = T.lb[:, 0:20]
-    tsc(T.e0[:], T.i64[:], col("pm"), 1024.0, [A.is_equal, A.mult], ["i64", "pm"], ["e0"])
-    tsc(T.e1[:], T.i64[:], col("pn"), -320.0, [A.is_equal, A.mult], ["i64", "pn"], ["e1"])
+    tsc(col("pa"), col("pc"), 15, None, [A.bitwise_and], ["pc"], ["pa"])
     cp(T.ul[:], T.ui[:], ["ui"], ["ul"])
-    tsc(col("fix0"), col("pa"), 15, 320.0, [A.is_lt, A.mult], ["pa"], ["fix0"])
+    tsc(col("mod"), col("pb"), 16, 2.0, [A.is_ge, A.mult], ["pb"], ["mod"])
+    for name, f, c in (("mev", -0.5, 1.0), ("wd", -0.25, 1.0), ("we", 0.25, 0.0)): affine(col(name), col("mod"), f, c, ["mod"], [name])
+    cp(col("pm"), col("pa"), ["pa"], ["pm"])
+    tsc(col("inv"), col("pa"), 15, 2.0 ** -16, [A.is_equal, A.max], ["pa"], ["inv"])
+    tsc(al, T.ai[:], col("pm"), None, [A.add], ["ai", "pm"], ["lb2"])
+    tsc(T.e0[:], T.i80[:, 16:80], col("pm"), None, [A.not_equal], ["i80", "pm"], ["e0"])
+    tsc(T.e1[:], T.i80[:, 15:79], col("pm"), 2.0 ** 16 - 1, [A.is_equal, A.mult], ["i80", "pm"], ["e1"])
+    cp(T.nf[:], T.lb[:, 0:40], ["lb0", "lb1"], ["nL", "pf"])
+    cp(T.lb[:, 160:180], T.lb[:, 20:40], ["lb1"], ["lb8"])
     tt(T.dv[:, 0:64], T.e0[:], T.e1[:], A.add, ["e0", "e1"], ["dv0"])
-    for i in range(1, 5): act(T.dv[:, 64 * i:64 * i + 64], T.dv[:, 0:64], ["dv0"], ["dv%d" % i])
+    for i in range(1, 5): dma("y", T.dv[:, 64 * i:64 * i + 64], T.dv[:, 0:64], ["dv0"], ["dv%d" % i])
+    act(row("nn"), idr.indirect(nL()), ["idr", "nL"], two("nn"))
     quant(T.uq[:], T.us[:], T.ut[:], ["ut"], ["uq"])
-    cp(T.nL[:], T.nx0[:], ["nx0"], ["nL"])
-    tsc(T.t1[:], T.lb[:, 0:80], col("mev"), None, [A.mult], ["lb0", "lb1", "lb2", "lb3", "mev"], ["t1"])
-    tsc(T.t2[:], T.lb[:, 80:160], col("mod"), None, [A.mult], ["lb4", "lb5", "lb6", "lb7", "mod"], ["t2"])
+    tsc(T.t1[:], T.lb[:, 20:100], col("mev"), None, [A.mult], ["lb1", "lb2", "lb3", "lb4", "mev"], ["t1"])
+    tsc(T.t2[:], T.lb[:, 100:180], col("mod"), 0.5, [A.mult, A.mult], ["lb5", "lb6", "lb7", "lb8", "mod"], ["t2"])
     cp(T.uu[:, 0:128].bitcast(dt.uint32), T.uq[:].bitcast(dt.uint32).indirect(T.ul[:, 0:8]), ["uq", "ul"], ["uu0"])
-    act(T.uus[:, 0:128], T.us[:].indirect(T.ul[:, 0:8]), ["uq", "ul"], ["uus0"])
-    act(row("nn"), row("idr").indirect(T.nL[:]), ["idr", "nL"], two("nn"))
+    for i in (0, 1): act(T.uus[:, 128 * i:128 * i + 128], T.us[:].indirect(T.ul[:, 8 * i:8 * i + 8]), ["uq", "ul"], ["uus%d" % i])
     tt(T.bl[:], T.t1[:], T.t2[:], A.add, ["t1", "t2"], ["bl"])
     tquant("xin", 0, ["xin0"])
-    cp(T.l1[:], T.bl[:, 0:20], ["bl"], ["l1"])
-    cp(T.pe[:], T.bl[:, 40:60], ["bl"], ["pe"])
+    cp(T.lp[:], T.bl[:, 0:40], ["bl"], ["pe", "l1"])
     tquant("xin", 1, ["xin1"])
     cp(T.uu[:, 128:256].bitcast(dt.uint32), T.uq[:].bitcast(dt.uint32).indirect(T.ul[:, 8:16]), ["uq", "ul"], ["uu1"])
-    act(T.uus[:, 128:256], T.us[:].indirect(T.ul[:, 8:16]), ["uq", "ul"], ["uus1"])
+    tsc(T.me3[:], T.bl[:, 40:60], 3.0, 2.0, [A.mult, A.add], ["bl"], ["me3"])
 
-    def ahead_r(keys): act(row("rr"), row("nn").indirect(T.l1[:]), two("nn") + keys, ["rr"])
-    def ahead_rp(): act(T.r3[:, 0:960:3], row("rr").indirect(T.pe[:]), ["rr", "pe"], ["r3a"])
-    def ahead_neg(): tsc(T.r3[:, 1:960:3], row("rr"), -1.0, None, [A.mult], ["rr"], ["r3b"])
-    def ahead_pos(): gcopy(T.r3[:, 2:960:3], row("rr"), C, ["rr"], ["r3c"])
+    def ahead_r(keys): act(row("rr"), row("nn").indirect(T.lp[:, 20:40]), two("nn") + keys, ["rr"])
+    def ahead_rp(): act(T.r3[:, 1:960:3], row("rr").indirect(T.lp[:, 0:20]), ["rr", "pe"], ["r3b"])
+    def ahead_copy(i): gcopy(T.r3[:, 2 * i:960:3], row("rr"), C, ["rr"], ["r3" + "ac"[i]])
 
-    def turn_tables():
-        tt(T.dd[:], T.lb[:, 40:60], al, A.subtract, ["lb2", "lb0"], ["dd"])
-        cp(T.xb[:, 2:60:3], T.bl[:, 60:80], ["bl"], ["xb2"])
-        tsc(T.me3[:], T.bl[:, 20:40], 3.0, 2.0, [A.mult, A.add], ["bl"], ["me3"])
-        tsc(T.xb[:, 1:60:3], T.dd[:], col("mod"), None, [A.mult], ["dd", "mod"], ["xb1"])
+    def terms_u(u, f0, f3, r):
+        for i, f in ((0, f0), (3, f3)): emit("s", lambda e: e.activation(T.xb[:, i:100:5], u, CP, scale=col(f)), r + [f], ["xb%d" % i])
 
-    def shift_tables():
-        tsc(col("fix3"), col("fix0"), 3.0, 482.0, [A.mult, A.add], ["fix0"], ["fix3"])
-        fill(T.tr[:, 32:48], 0.0, ["tr+"])
-        fill(T.sh[:, 20:40], 0, ["sh+1"])
-        tsc(T.sh[:, 0:20], al, 960.0, None, [A.add], ["lb0"], ["sh+0"])
+    def term_v(i, v, r):
+        if i == 1: tsc(T.xb[:, 1:100:5], v, col("sq"), -1.0, [A.mult, A.mult], r + ["sq"], ["xb1"])
+        else: tsc(T.xb[:, 4:100:5], v, col("we"), None, [A.mult], r + ["we"], ["xb4"])
 
     def unpackers(bs):
         for b in bs: quant(T["eq%d" % b][:], T["es%d" % b][:], T.et[:, 3 - b:515 - b], ["et"], ["eq%d" % b])
@@ -193,29 +190,45 @@ def rank_program(g, core, T, topo):
     def fmm(bs):
         for b in bs: mm(b, C, T["eq%d" % b][:], T["es%d" % b][:], T.tq[:], T.ts[:], ["eq%d" % b, "tq0", "tq1"])
 
-    def fcopy(b):
-        act(run("fw", b), bank(b, C), ["ps%d" % b], ["fw%d" % b], 2.0 if b > 1 else 1.0)
-        if b > 1: dma("y", run("f2", b - 2), run("fw", b), ["fw%d" % b], ["f2%d" % b])
+    def fcopy(bs):
+        for b in bs:
+            act(run("fw", b), bank(b, C), ["ps%d" % b], ["fw%d" % b], 2.0 if b > 1 else 1.0)
+            if b > 1: dma("y", run("f2", b - 2), run("fw", b), ["fw%d" % b], ["f2%d" % b])
 
-    def layer(h, b0):
+    def mean(b, h):
+        out, n, w = T.zt[:, 640 * h + b:640 * h + 640:4], nL(10 * h, 10 * h + 10), ["zt%d.%d" % (h, b)]
+        if b > 1: act(out, run("yw", b - 2).indirect(n), ["yw%d" % b, "nL"], w, 0.5)
+        else: tt(out, run("gw", b).indirect(n), run("g2", b, HF * h, HF * h + HF), A.add, ["gw%d" % b, "g2%d.%d" % (b, h), "nL"], w)
+
+    def layer(h):
         c = slice(HF * h, HF * h + HF)
+        quant(T.zq[:, c], T.zs[:, c], T.zt[:, 640 * h:640 * h + 640], ["zt%d.%d" % (h, b) for b in range(4)], ["zq%d" % h])
         for b in range(4):
-            mm(b0 + b, HF, T.wq[:, 128 * b:128 * b + 128], T.wsp[:, 128 * b:128 * b + 128], T.zq[:, c], T.zs[:, c], ["wq", "wsp", "zq%d" % h])
+            mm(4 * h + b, HF, T.wq[:, 128 * b:128 * b + 128], T.wsp[:, 128 * b:128 * b + 128], T.zq[:, c], T.zs[:, c], ["wq", "wsp", "zq%d" % h])
 
-    def htile(tile, b0):
-        for b in range(4):
-            act(T[tile][:, b:640:4], bank(b0 + b, HF), ["ps%d" % (b0 + b)], ["%s.%d" % (tile, b)], 0.03125)
+    def htile(on, tile, b0, bs):
+        for b in bs:
+            out, r, w = T[tile][:, b:640:4], ["ps%d" % (b0 + b)], ["%s.%d" % (tile, b)]
+            if on == "s": act(out, bank(b0 + b, HF), r, w, 0.03125)
+            else: tsc(out, bank(b0 + b, HF), 0.03125, None, [A.mult], r, w)
 
     def pack(tile, hq, hs): quant(T[hq][:], T[hs][:], T[tile][:], ["%s.%d" % (tile, b) for b in range(4)], [hq])
 
-    def unpack(hq, hs, b0):
-        for b in (2, 0, 3, 1):
-            mm(b0 + b, HF, T["eq%d" % b][:], T["es%d" % b][:], T[hq][:], T[hs][:], ["eq%d" % b, hq])
+    def unpack(hq, hs, b0, bs):
+        for b in bs: mm(b0 + b, HF, T["eq%d" % b][:], T["es%d" % b][:], T[hq][:], T[hs][:], ["eq%d" % b, hq])
 
     def xsum(h, b0, b): tt(run("xw", b, HF * h, HF * h + HF), run("gw", b, HF * h, HF * h + HF), bank(b0 + b, HF), A.add, ["gw%d" % b, "ps%d" % (b0 + b)], ["xw%d.%d" % (b, h)])
 
     def kcopy(h, b0):
         for b in (2, 3): act(run("kw", b - 2, HF * h, HF * h + HF), bank(b0 + b, HF), ["ps%d" % (b0 + b)], ["kw%d.%d" % (b, h)], 2.0)
+
+    def invert(lo, hi): cp(run("mr", 0).indirect(nL(lo, hi)), T.w2[:, 640 + 16 * lo:640 + 16 * hi], ["idr", "nL"], ["mr"])
+
+    def state(b, h):
+        lo, hi = CUT[h]
+        out, m, w = T.xst[:, 4 * lo + b:4 * hi:4], T.mL[:, lo // 16:hi // 16], ["xst%d.%d" % (h, b)]
+        if b < 2: act(out, run("xw", b).indirect(m), ["xw%d.0" % b, "xw%d.1" % b, "mL"], w, 2.0)
+        else: tt(out, run("kw", b - 2).indirect(m), run("fw", b, lo, hi), A.add, ["kw%d.0" % b, "kw%d.1" % b, "fw%d" % b, "mL"], w)
 
     def send(k, partner):
         rid, pid, _ = topo.addr(partner)
@@ -228,157 +241,156 @@ def rank_program(g, core, T, topo):
         note(("remote", "arr%d" % k, n, {}), [], ["lq%d" % k])
         moved.append((k, n))
 
-    def cross(out, src, up, r, w):
+    def cross(name, at, src, up, r, w):
         for a in range(4):
             lo, hi = slice(32 * a, 32 * a + 16), slice(32 * a + 16, 32 * a + 32)
-            dma("y", T[out][lo if up else hi, :], T[src][hi if up else lo, :], r, ["%s%d" % (w, a)])
+            dma("y", T[name][lo if up else hi, at:at + 20], T[src][hi if up else lo, 0:20], r, ["%s%d" % (w, a)])
 
-    def products(h):
+    def product(i, h):
         lo, hi = CUT[h]
-        for i in (0, 1): mm(4 + 2 * i + h, hi - lo, T.uu[:, 128 * i:128 * i + 128], T.uus[:, 128 * i:128 * i + 128], T.tq[:, lo:hi], T.ts[:, lo:hi], ["uu%d" % i, "uus%d" % i, "tq%d" % h])
+        mm(4 + 2 * i + h, hi - lo, T.uu[:, 128 * i:128 * i + 128], T.uus[:, 128 * i:128 * i + 128], T.tq[:, lo:hi], T.ts[:, lo:hi], ["uu%d" % i, "uus%d" % i, "tq%d" % h])
 
     def signs(on, name, h):
         lo, hi = CUT[h]
         b = 4 + 2 * (name == "sf") + h
-        if on == "v": tsc(T[name][:, lo:hi], bank(b, hi - lo), 0.0, None, [A.is_gt], ["ps%d" % b], [name + "%d" % h])
+        if on == "v": tsc(T[name][:, lo:hi], bank(b, hi - lo), 0.0, 0.5, [A.is_gt, A.subtract], ["ps%d" % b], [name + "%d" % h])
         else: emit("s", lambda e: e.activation(T[name][:, lo:hi], bank(b, hi - lo), SG, bias=-(2.0 ** -93)), ["ps%d" % b], [name + "%d" % h])
 
     def agree(h):
         lo, hi = CUT[h]
-        tt(T.c3[:, 3 * lo + 2:3 * hi:3], row("sa").indirect(T.pe[:, lo // 16:hi // 16]), T.sb_[:, lo:hi], A.is_equal, two("sa") + ["sb_%d" % h, "pe"], ["c3c%d" % h])
+        tt(T.c3[:, 3 * lo + 2:3 * hi:3], row("sa").indirect(T.lp[:, lo // 16:hi // 16]), T.sb_[:, lo:hi], A.is_equal, two("sa") + ["sb_%d" % h, "pe"], ["c3c%d" % h])
 
     def choose(h):
         c = slice(3 * CUT[h][0], 3 * CUT[h][1])
-        scan(T.fo[:, c], T.c3[:, c], T.r3[:, c], [A.mult, A.add], ["c3a", "c3b", "c3c%d" % h, "r3a", "r3b", "r3c"], ["fo%d" % h])
+        scan(T.fo[:, c], T.c3[:, c], T.r3[:, c], ["c3a", "c3b", "c3c%d" % h, "r3a", "r3b", "r3c"], ["fo%d" % h])
+    FO = two("fo")
+
+    def own_signs(h):
+        lo, hi = CUT[h]
+        scan(T.q5[:, 5 * lo:5 * hi:5], T.dv[:, lo:hi], T.sf[:, lo:hi], DV + ["sf%d" % h], ["q5c%d" % h])
+
+    def pair_signs(): scan(T.q5[:, 16:1616:5], row("dv"), row("spf"), DV + ["spf"], ["q5d"])
+    def choice(): scan(T.qo[:], T.q5[:, 43:1632:16], T.xb[:], ["xb%d" % i for i in range(5)] + ["q5a", "q5b", "q5c0", "q5c1", "q5d", "q5e"], ["qo"])
+
+    def onward(i, f, base):
+        for a in range(4):
+            c = 32 * ((a + 1) % 4)
+            tsc(T.sh[c:c + 16, 20 * i:20 * i + 20], T.tb[32 * a:32 * a + 16, 16 * i:640:32], f, base, [A.mult, A.add], two("tb") + ["sh+"], ["sh%d.%d" % (i, a)])
 
     moved = []
-    products(0)
-    products(1)
+    for i, h in ((0, 0), (0, 1), (1, 0), (1, 1)): product(i, h)
     ahead_r(["l1"])
-    cp(T.pf[:], T.lb[:, 40:60], ["lb2"], ["pf"])
-    signs("v", "sa", 0)
-    signs("v", "sb_", 0)
-    signs("v", "sa", 1)
-    signs("v", "sb_", 1)
-    ahead_pos()
-    count(T.w2[:, 0:960], [[0, 960]], 0, two("rw"))
-    signs("s", "sf", 0)
+    for name, h in (("sa", 0), ("sa", 1), ("sb_", 0), ("sb_", 1)): signs("s", name, h)
+    ahead_copy(0)
+    gg(lambda e: e.iota(T.aj[:], [[0, 2], [16, 2], [32, 10]], C, 0), [], ["aj"])
+    count(run("mr", 1), [[0, C]], 0, ["mr2"])
+    count(T.mG[:], [[0, 20]], 0, ["mG"])
     ahead_rp()
-    signs("s", "sf", 1)
-    turn_tables()
+    tsc(col("sq"), col("inv"), col("inv"), col("mod"), [A.mult, A.mult], ["inv", "mod"], ["sq"])
+    term_v(4, al, ["lb2"])
+    unpackers((2, 3))
+    term_v(1, al, ["lb2"])
+    signs("v", "sf", 0)
+    cp(T.r3[:, 2:960:3], row("rr"), ["rr"], ["r3c"])
+    signs("v", "sf", 1)
+    for h in (0, 1): own_signs(h)
     for k in range(ROUNDS):
         last = k == ROUNDS - 1
         partner = T.cores[rank ^ STEP[k]]
-        act(row("spf"), row("sf").indirect(T.pf[:]), two("sf") + ["pf"], ["spf"])
-        if k: fmm((2, 3, 0, 1))
-        agree(0)
-        if k == 0: ahead_neg()
-        agree(1)
-        if k == 0: pick("q1", row("sf"), two("sf"))
-        choose(0)
-        pick("q2", row("spf"), ["spf"])
-        choose(1)
+        act(row("spf"), row("sf").indirect(T.nf[:, 20:40]), two("sf") + ["pf"], ["spf"])
+        for h in (0, 1): agree(h)
         if k:
-            fcopy(2)
-        tt(T.qb[:, 1:60:3], ends("q1"), ends("q2"), A.is_equal, ["q1", "q2"], ["qb1"])
-        ME = ["me3"] + (four("me3") if k else [])
-        act(T.b2[:, 128:C], row("fo").indirect(T.me3[:, 8:20]), two("fo") + ME, ["b21"])
-        if k == 0: unpackers((2,))
-        scan(T.qo[:], T.xb[:], T.qb[:], [A.add, A.mult], ["xb0", "xb1", "xb2", "qb0", "qb1", "qb2"], ["qo"])
-        cp(T.b2[:, 0:128], row("fo").indirect(T.me3[:, 0:8]), two("fo") + ME, ["b20"])
-        cp(T.l3[:], T.qo[:, 2:60:3], ["qo"], ["l3"])
-        if k == 0: unpackers((3,))
-        split("w2", 960, 1, row("b2"), "l3", 0, two("b2") + ["l3"], "nm")
-        if k == 0:
-            shift_tables()
-            fmm((2, 3))
-            fcopy(2)
-        fcopy(3)
-        pick("sc", T.w2[:, 960:1280], two("nm"))
-        if k == 0: unpackers((0,))
-        turn(T.tr[:, 0:32], T.sc[:, 15:527:16], ["sc", "sc+"], ["tr"])
-        if k == 0: unpackers((1,))
-        turn(T.sc[:, 335:847:16], T.tr[:, 16:48], ["tr", "tr+"], ["sc+"])
-        if k == 0:
-            fmm((0, 1))
-            cp(T.mf[:], al, ["lb0"], ["mf"])
-        fcopy(0)
-        if k: fcopy(1)
-        for a in range(4):
-            c = 32 * ((a + 1) % 4)
-            tsc(T.sh[c:c + 16, :], T.sc[32 * a:32 * a + 16, 15:655:16], 3.0, T.fix3[32 * a:32 * a + 16, 0:1], [A.mult, A.add], ["sc", "sc+", "fix3", "sh+0", "sh+1"], ["sh%d" % a])
-        SH = four("sh") + two("sh+")
-        split("w2", 2, 3, row("fo"), "sh", 20, two("fo") + SH, "rw")
-        split("nn", 0, 1, row("w2"), "sh", 0, two("rw") + two("nm") + SH, "nn")
-        if k == 0: fcopy(1)
-        pick("sn", row("nn"), two("nn"))
-        if k == 0: quant(T.vq[:], T.vs[:], T.vt[:], ["vt"], ["vq"])
-        tolist("nL", "sn")
-        if not last: cross("l1", "nL", False, ["nL"], "l1")
+            fmm((2, 3, 0, 1))
+            terms_u(ends("su"), "ua", "ub", ["su"])
+            fcopy((2, 3))
+            pair_signs()
+            choose(0)
+            choice()
+            choose(1)
         else:
-            emit("s", lambda e: e.activation(row("nlf"), row("nn"), ActivationFunctionType.Identity, bias=160.0), two("nn"), ["nlf"])
+            fmm((2, 3))
+            terms_u(T.bl[:, 60:80], "sq", "wd", ["bl"])
+            for h in (0, 1): choose(h)
+            part("s", "b2", 0, row("fo"), "me3", 0, 4, 20, FO + ["me3"], "b21")
+            fcopy((2,))
+            pair_signs()
+            part("v", "b2", 0, row("fo"), "me3", 0, 0, 4, FO + ["me3"], "b20")
+            choice()
+            unpackers((0,))
+        for i in (0, 1):
+            tsc(T.l3[:, i:20:2], T.qo[:, 4 + 50 * i:50 + 50 * i:5], 3.0 if k else 1.0, 482.25 if k else 0.25, [A.mult, A.add], ["qo"], ["l3%d" % i])
+        if k:
+            split("w2", C, row("fo"), "l3", 0, FO + two("l3"), "nm")
+            fcopy((0, 1))
+        else:
+            unpackers((1,))
+            split("w2", C, row("b2"), "l3", 0, two("b2") + two("l3"), "nm")
+            tsc(T.sh[:], T.aj[:], col("pm"), None, [A.add], ["aj", "pm"], ["sh+"])
+            fmm((0, 1))
+            fcopy((3, 0))
+        for i in (0, 1): turn(T.tb[:, C * i:C * i + C], T.w2[:, C + 16 * i:640 + 16 * i], two("nm") + ["idr"], ["tb%d" % i])
+        if k == 0: tsc(T.l4[:], T.nf[:, 20:40], 320.0, None, [A.add], ["pf"], ["l4"])
+        onward(1, 3.0, 482.0)
+        part("s", "w2", 0, row("fo"), "sh", 20, 8, 20, FO + four("sh1."), "rw1")
+        onward(0, 1.0, 160.0)
+        part("v", "w2", 0, row("fo"), "sh", 20, 0, 8, FO + four("sh1."), "rw0")
+        split("nn", 0, T.w2[:, 0:640], "sh", 0, two("rw") + two("nm") + four("sh0."), "nn")
+        if k == 0:
+            fcopy((1,))
+            for f, w in (("ua", "sq"), ("ub", "wd")): tsc(col(f), col("inv"), col(w), None, [A.mult], ["inv", w], [f])
+        pick("sn", "nn", two("nn"))
+        if k == 0: quant(T.vq[:], T.vs[:], T.vt[:], ["vt"], ["vq"])
+        tolist(nL(), "sn", "nL")
+        if not last: cross("lp", 20, "nf", False, ["nL", "l1"], "l1")
+        else:
+            affine(row("nlf"), row("nn"), 1.0, 160.0, two("nn"), ["nlf"])
             dma("y", T.nl[:], T.nlf[0:128:16, :], ["nlf"], [])
-        for b in (0, 1): act(run("gw", b), run("fw", b).indirect(T.nL[:]), ["fw%d" % b, "nL"], ["gw%d" % b])
-        for b in (2, 3): tt(run("yw", b - 2), run("fw", b).indirect(T.nL[:]), run("f2", b - 2), A.add, ["fw%d" % b, "f2%d" % b, "nL"], ["yw%d" % b])
+        for b in (0, 1): act(run("gw", b), run("fw", b).indirect(nL()), ["fw%d" % b, "nL"], ["gw%d" % b])
+        for b in (2, 3): tt(run("yw", b - 2), run("fw", b).indirect(nL()), run("f2", b - 2), A.add, ["fw%d" % b, "f2%d" % b, "nL"], ["yw%d" % b])
         for b in (0, 1): gcopy(run("g2", b, 0, HF), run("gw", b, 0, HF), HF, ["gw%d" % b], ["g2%d.0" % b])
-        for h in (1, 0):
-            n = T.nL[:, 10 * h:10 * h + 10]
-            for b in (2, 3): act(T.zt[:, 640 * h + b:640 * h + 640:4], run("yw", b - 2).indirect(n), ["yw%d" % b, "nL"], ["zt%d.%d" % (h, b)], 0.5)
-            if h:
-                for b in (0, 1): cp(run("g2", b, HF), run("gw", b, HF), ["gw%d" % b], ["g2%d.1" % b])
-            for b in (0, 1): tt(T.zt[:, 640 * h + b:640 * h + 640:4], run("gw", b).indirect(n), run("g2", b, HF * h, HF * h + HF), A.add, ["gw%d" % b, "g2%d.%d" % (b, h), "nL"], ["zt%d.%d" % (h, b)])
-            c = slice(HF * h, HF * h + HF)
-            quant(T.zq[:, c], T.zs[:, c], T.zt[:, 640 * h:640 * h + 640], ["zt%d.%d" % (h, b) for b in range(4)], ["zq%d" % h])
-            layer(h, 4 * h)
-        def invert(lo, hi): cp(row("mr").indirect(T.nL[:, lo:hi]), T.idr[:, 16 * lo:16 * hi], ["idr", "nL"], ["mr"])
-        htile("hp", 4)
+        for b in (0, 1): cp(run("g2", b, HF), run("gw", b, HF), ["gw%d" % b], ["g2%d.1" % b])
+        for b, h in ((2, 1), (3, 1), (2, 0), (3, 0), (0, 1), (1, 1), (0, 0)): mean(b, h)
+        layer(1)
+        mean(1, 0)
+        layer(0)
+        if not last: ahead_r(four("l1"))
+        htile("s", "hp", 4, (0, 1, 3))
+        htile("v", "hp", 4, (2,))
         invert(0, 4)
         pack("hp", "hqp", "hsp")
         send(k, partner)
-        htile("ho", 0)
-        invert(4, 12)
+        htile("s", "ho", 0, (0, 2, 3))
+        htile("v", "ho", 0, (1,))
+        invert(4, 10)
         pack("ho", "hqo", "hso")
-        unpack("hqo", "hso", 4)
-        invert(12, 20)
+        unpack("hqo", "hso", 4, (0, 2, 1, 3))
+        invert(10, 20)
         if not last:
-            ahead_r(["l1"] + four("l1"))
-            ahead_pos()
-        unpack("lq%d" % k, "ls%d" % k, 0)
+            for i in (0, 1): ahead_copy(i)
+            ahead_rp()
+            dma("y", T.mr[16:128, C:640], T.mr[0:112, 0:C], ["mr"], ["mr2"])
+        unpack("lq%d" % k, "ls%d" % k, 0, (2, 0, 1, 3))
         kcopy(0, 4)
         xsum(0, 4, 0)
-        pick("sm", row("mr"), ["mr"])
+        pick("sm", "mr", ["mr"])
         xsum(0, 4, 1)
-        tolist("mL", "sm")
+        tolist(row("mL"), "sm", "mL")
+        if not last:
+            cross("l4", 0, "mL", True, ["mL", "l4"], "l4")
+            tsc(T.mF[:], ends("sm"), col("inv"), None, [A.mult], ["sm", "inv"], ["mF"])
+            dma("y", T.mG[16:128, :], T.mF[0:112, :], ["mF"], ["mG"])
         kcopy(1, 0)
-        xsum(1, 0, 0)
+        for b in (0, 1): xsum(1, 0, b)
+        for b, h in ((2, 0), (2, 1), (3, 0), (3, 1), (0, 0), (1, 0), (1, 1), (0, 1)): state(b, h)
+        if not last: act(row("ur"), row("mr").indirect(T.l4[:]), ["mr", "mr2"] + four("l4"), ["ur"])
+        for h in (0, 1): tquant("xst", h, ["xst%d.%d" % (h, b) for b in range(4)])
         if not last:
-            tsc(T.me3[:], ends("sm"), 3.0, col("fix3"), [A.mult, A.add], ["sm", "fix3"], ["me3"] + four("me3"))
-            cross("me3", "me3", False, ["me3"], "me3")
-            cross("mf", "mL", True, ["mL", "mf"], "mf")
-        xsum(1, 0, 1)
-
-        def state(b, h):
-            lo, hi = CUT[h]
-            out, m, w = T.xst[:, 4 * lo + b:4 * hi:4], T.mL[:, lo // 16:hi // 16], ["xst%d.%d" % (h, b)]
-            if b < 2: act(out, run("xw", b).indirect(m), ["xw%d.0" % b, "xw%d.1" % b, "mL"], w, 2.0)
-            else: tt(out, run("kw", b - 2).indirect(m), run("fw", b, lo, hi), A.add, ["kw%d.0" % b, "kw%d.1" % b, "fw%d" % b, "mL"], w)
-
-        def squant(h): tquant("xst", h, ["xst%d.%d" % (h, b) for b in range(4)])
-        for b, h in ((0, 0), (1, 0), (0, 1), (1, 1), (2, 0), (3, 0), (2, 1)): state(b, h)
-        squant(0)
-        if not last:
-            products(0)
-            ahead_rp()
-        state(3, 1)
-        squant(1)
-        if not last:
-            products(1)
-            signs("v", "sf", 0)
-            ahead_neg()
+            for i, h in ((0, 0), (1, 0), (1, 1), (0, 1)): product(i, h)
+            for i in (1, 4): term_v(i, T.mG[:], ["mG"])
+            for h in (0, 1): signs("v", "sf", h)
             for name, h in (("sa", 0), ("sb_", 0), ("sa", 1), ("sb_", 1)): signs("s", name, h)
-            signs("v", "sf", 1)
-            cp(T.xb[:, 2:60:3], T.mf[:], four("mf"), ["xb2"])
-            pick("q1", row("sf"), two("sf"))
+            pick("su", "ur", ["ur"])
+            for h in (0, 1): own_signs(h)
 
     for h in (0, 1):
         lo, hi = CUT[h]

from concourse.mybir import dt, AluOpType, ActivationFunctionType
import comms_topo

C, HF = 320, 160
T0 = 192
ROUNDS = 3
STEP = [1, 2, 4]
BF, F32, I32, U16, U8, MXC = "bfloat16", "float32", "int32", "uint16", "uint8", "float8_e4m3fn_x4"


def _scratch():
    s = {}

    def sb(dtype, **kw):
        for k, n in kw.items():
            s[k] = ("sbuf", [128, n], dtype)
    sb(BF, xin=1280, xst=1280, zt=1280, ho=640, hp=640, ut=512, vt=512, et=516)
    sb(BF, fw=1280, f2=640, gw=640, g2=640, yw=640, xw=640, kw=640)
    sb(BF, dv=C, sa=C, sb_=C, sf=C, spf=C, c3=960, r3=960, fo=960, b2=C, w2=960, tb=640, nn=C, rr=C, mr=640, ur=C)
    sb(BF, q5=1632, sn=C, sm=C, su=C)
    sb(F32, yo=C, nlf=C, i80=80, e0=64, e1=64, pm=2, mev=2, wd=2, we=2, mod=2, inv=2, sq=2, ua=2, ub=2)
    sb(F32, t1=80, t2=80, bl=80, xb=100, qo=100, mF=20, mG=20)
    sb(I32, lb=180, pc=2, pa=2, pb=2, ai=20, aj=40, ui=16)
    sb(U16, lp=40, nf=40, me3=20, l4=20, l3=20, sh=40, mL=20, ul=16)
    sb(MXC, tq=C, zq=C, hqo=HF, hqp=HF, uq=128, uu=256, vq=128, wq=512, eq0=128, eq1=128, eq2=128, eq3=128)
    sb(U8, ts=C, zs=C, hso=HF, hsp=HF, us=128, uus=256, vs=128, wsp=512, es0=128, es1=128, es2=128, es3=128)
    for k in range(ROUNDS):
        s["lq%d" % k] = ("sbuf", [128, HF], MXC)
        s["ls%d" % k] = ("sbuf", [128, HF], U8)
    s["ps"] = ("psum", [128, 512 * 8], F32)
    return s


SCRATCH = _scratch()
SEMAPHORES = ["qv", "qs", "qp", "qg"] + ["arr%d" % k for k in range(ROUNDS)] + ["loc%d" % k for k in range(ROUNDS)] + ["dm%d" % k for k in range(64)]


def rank_program(g, core, T, topo):
    rank = T.rank_of(core)
    if rank is None:
        return
    A = AluOpType
    CP, ID, SG = ActivationFunctionType.Copy, ActivationFunctionType.Identity, ActivationFunctionType.Sign
    V, S, P = g.vector, g.scalar, g.tensor
    queue = {"v": V, "s": S, "p": P, "g": g, "y": g.sync}
    semof = {"v": "qv", "s": "qs", "p": "qp", "g": "qg"}
    cnt = {}
    known = {q: {} for q in queue}
    writer, readers, ndma = {}, {}, [0]

    def need(q, tok):
        if known[q].get(tok[1], 0) < tok[2]:
            queue[q].wait_ge(T.sem[tok[1]], tok[2])
            known[q][tok[1]] = tok[2]
        for k, n in tok[3].items():
            if known[q].get(k, 0) < n: known[q][k] = n

    def order(q, who, reads, writes):
        toks = []
        for k in reads:
            if k in writer: toks.append(writer[k])
            if k[:2] == "ps": toks += [t for t in readers.get(k, []) if t[0] != who]
        for k in writes:
            if k in writer and (writer[k][0] != who or who != "p"): toks.append(writer[k])
            toks += [t for t in readers.get(k, []) if t[0] != who]
        for t in sorted(toks, key=lambda t: -t[2]): need(q, t)

    def note(tok, reads, writes):
        for k in reads: readers.setdefault(k, []).append(tok)
        for k in writes:
            writer[k] = tok
            readers[k] = []

    def emit(q, fn, reads, writes):
        order(q, q, reads, writes)
        s = semof[q]
        cnt[s] = cnt.get(s, 0) + 1
        fn(queue[q]).then_inc(T.sem[s], 1)
        note((q, s, cnt[s], dict(known[q])), reads, writes)

    def dma(q, out, in_, reads, writes):
        s = "dm%d" % ndma[0]
        ndma[0] += 1
        order(q, s, reads, writes)
        queue[q].dma_start(out, in_).then_inc(T.sem[s], 16)
        note((s, s, 16, dict(known[q])), reads, writes)

    def vv(fn, r, w): emit("v", fn, r, w)
    def gg(fn, r, w): emit("g", fn, r, w)
    def fill(ap, c, w): vv(lambda e: e.memset(ap, c), [], w)
    def tt(out, in0, in1, op, r, w): vv(lambda e: e.tensor_tensor(out, in0, in1, op), r, w)
    def tsc(out, in0, s1, s2, ops, r, w): vv(lambda e: e.tensor_scalar(out, in0, s1, s2, *ops), r, w)
    def cp(out, in_, r, w): vv(lambda e: e.tensor_copy(out, in_), r, w)
    def act(out, in_, r, w, scale=1.0): emit("s", lambda e: e.activation(out, in_, CP) if scale == 1.0 else e.activation(out, in_, CP, scale=scale), r, w)
    def affine(out, in_, scale, bias, r, w): emit("s", lambda e: e.activation(out, in_, ID, bias=bias, scale=scale), r, w)
    def quant(c, s, t, r, w): vv(lambda e: e.quantize_mx(c, s, t), r, w)
    def scan(out, d, x, r, w): vv(lambda e: e.tensor_tensor_scan(out, d, x, 0.0, A.mult, A.add), r, w)
    def turn(out, in_, r, w): vv(lambda e: e.transpose(out, in_), r, w)
    def count(out, pattern, base, w): gg(lambda e: e.iota(out, pattern, base, 0, allow_small_or_imprecise_dtypes=True), [], w)
    def gcopy(out, in_, n, r, w): gg(lambda e: e.affine_select(out, in_, [[0, n]], A.is_ge, 0.0, 0, 0), r, w)

    def mm(bank, n, a, sa, b, sb, r):
        emit("p", lambda e: e.matmul_mx(T.ps[:, 512 * bank:512 * bank + n], a, sa, b, sb, True, True), r, ["ps%d" % bank])

    def bank(i, n): return T.ps[:, 512 * i:512 * i + n]
    def row(name): return T[name][:]
    def ends(name): return T[name][:, 15:C:16]
    def col(name): return T[name][:, 0:1]
    def run(name, i, lo=0, hi=C): return T[name][:, C * i + lo:C * i + hi]
    def two(name): return [name + "0", name + "1"]
    def four(name): return [name + "%d" % a for a in range(4)]
    def nL(a=0, b=20): return T.nf[:, a:b]
    DV = ["dv%d" % i for i in range(5)]
    def pick(out, x, r): scan(row(out), row("dv"), run(x, 0), DV + r, [out])
    def tolist(out, sc, w): tsc(out, ends(sc), col("inv"), 160.25, [A.mult, A.add], [sc, "inv"], [w])
    CUT = ((0, T0), (T0, C))
    def tquant(tile, h, r): quant(T.tq[:, CUT[h][0]:CUT[h][1]], T.ts[:, CUT[h][0]:CUT[h][1]], T[tile][:, 4 * CUT[h][0]:4 * CUT[h][1]], r, ["tq%d" % h])

    def part(on, out, at, w, lst, lo, a, b, r, wr):
        (cp if on == "v" else act)(T[out][:, at + 16 * a:at + 16 * b], w.indirect(T[lst][:, lo + a:lo + b]), r, [wr])

    def split(out, at, w, lst, lo, r, wr, cut=10):
        part("v", out, at, w, lst, lo, 0, cut, r, wr + "0")
        part("s", out, at, w, lst, lo, cut, 20, r, wr + "1")

    fill(T.lb[:, 80:160], 0, ["lb4", "lb5", "lb6", "lb7"])
    fill(T.et[:], 0.5, ["et"])
    dma("y", T.ut[:], T.u[:], [], ["ut"])
    dma("s", T.lb[:, 0:20], T.nx[:], [], ["lb0"])
    dma("y", T.xin[:, 0:4 * T0], T.x[:, 0:4 * T0], [], ["xin0"])
    dma("s", T.lb[:, 20:40], T.pr[:], [], ["lb1"])
    dma("y", T.xin[:, 4 * T0:1280], T.x[:, 4 * T0:1280], [], ["xin1"])
    dma("s", T.lb[:, 60:80], T.iv[:], [], ["lb3"])
    for i, src in enumerate((T.pr, T.nx, T.iv)): dma("sy"[i % 2], T.lb[16:128, 100 + 20 * i:120 + 20 * i], src[0:112, :], [], ["lb%d" % (5 + i)])
    dma("y", T.lb[0:112, 80:100], T.iv[16:128, :], [], ["lb4"])
    dma("y", T.wq[:].bitcast(dt.uint8), T.wc[:], [], ["wq"])
    dma("y", T.wsp[:], T.ws[:], [], ["wsp"])
    dma("y", T.vt[:], T.v[:], [], ["vt"])

    idr, al = T.w2[:, 640:960], T.lb[:, 40:60]
    gg(lambda e: e.iota(T.pc[:, 0:1], [[0, 1]], 0, 1), [], ["pc"])
    gg(lambda e: e.iota(T.ui[:], [[16, 2], [32, 4], [0, 2]], 0, 0), [], ["ui"])
    count(T.i80[:], [[0, 5], [1, 16]], 0, ["i80"])
    gg(lambda e: e.iota(T.ai[:], [[16, 20]], 0, 0), [], ["ai"])
    count(idr, [[1, C]], -160, ["idr"])
    for out, f, w in ((T.c3[:, 0:960:3], 0.0, "c3a"), (T.c3[:, 1:960:3], -2.0, "c3b")): act(out, T.et[:, 0:C], ["et"], [w], f)
    gg(lambda e: e.affine_select(T.et[:], T.et[:], [[-1, 516]], A.is_equal, 0.0, 3, 4), ["et"], ["et"])
    for out, v, w in ((T.q5[:, 43:1632:80], 0, "q5a"), (T.q5[:, 59:1632:80], 1, "q5b"), (T.q5[:, 107:1632:80], 1, "q5e"), (T.xb[:, 2:100:5], 0, "xb2")): count(out, [[0, 20]], v, [w])
    tsc(col("pb"), col("pc"), 31, None, [A.bitwise_and], ["pc"], ["pb"])
    tsc(col("pa"), col("pc"), 15, None, [A.bitwise_and], ["pc"], ["pa"])
    cp(T.ul[:], T.ui[:], ["ui"], ["ul"])
    tsc(col("mod"), col("pb"), 16, 2.0, [A.is_ge, A.mult], ["pb"], ["mod"])
    for name, f, c in (("mev", -0.5, 1.0), ("wd", -0.25, 1.0), ("we", 0.25, 0.0)): affine(col(name), col("mod"), f, c, ["mod"], [name])
    cp(col("pm"), col("pa"), ["pa"], ["pm"])
    tsc(col("inv"), col("pa"), 15, 2.0 ** -16, [A.is_equal, A.max], ["pa"], ["inv"])
    tsc(al, T.ai[:], col("pm"), None, [A.add], ["ai", "pm"], ["lb2"])
    tsc(T.e0[:], T.i80[:, 16:80], col("pm"), None, [A.not_equal], ["i80", "pm"], ["e0"])
    tsc(T.e1[:], T.i80[:, 15:79], col("pm"), 2.0 ** 16 - 1, [A.is_equal, A.mult], ["i80", "pm"], ["e1"])
    cp(T.nf[:], T.lb[:, 0:40], ["lb0", "lb1"], ["nL", "pf"])
    cp(T.lb[:, 160:180], T.lb[:, 20:40], ["lb1"], ["lb8"])
    tt(T.dv[:, 0:64], T.e0[:], T.e1[:], A.add, ["e0", "e1"], ["dv0"])
    for i in range(1, 5): dma("y", T.dv[:, 64 * i:64 * i + 64], T.dv[:, 0:64], ["dv0"], ["dv%d" % i])
    act(row("nn"), idr.indirect(nL()), ["idr", "nL"], two("nn"))
    quant(T.uq[:], T.us[:], T.ut[:], ["ut"], ["uq"])
    tsc(T.t1[:], T.lb[:, 20:100], col("mev"), None, [A.mult], ["lb1", "lb2", "lb3", "lb4", "mev"], ["t1"])
    tsc(T.t2[:], T.lb[:, 100:180], col("mod"), 0.5, [A.mult, A.mult], ["lb5", "lb6", "lb7", "lb8", "mod"], ["t2"])
    cp(T.uu[:, 0:128].bitcast(dt.uint32), T.uq[:].bitcast(dt.uint32).indirect(T.ul[:, 0:8]), ["uq", "ul"], ["uu0"])
    for i in (0, 1): act(T.uus[:, 128 * i:128 * i + 128], T.us[:].indirect(T.ul[:, 8 * i:8 * i + 8]), ["uq", "ul"], ["uus%d" % i])
    tt(T.bl[:], T.t1[:], T.t2[:], A.add, ["t1", "t2"], ["bl"])
    tquant("xin", 0, ["xin0"])
    cp(T.lp[:], T.bl[:, 0:40], ["bl"], ["pe", "l1"])
    tquant("xin", 1, ["xin1"])
    cp(T.uu[:, 128:256].bitcast(dt.uint32), T.uq[:].bitcast(dt.uint32).indirect(T.ul[:, 8:16]), ["uq", "ul"], ["uu1"])
    tsc(T.me3[:], T.bl[:, 40:60], 3.0, 2.0, [A.mult, A.add], ["bl"], ["me3"])

    def ahead_r(keys): act(row("rr"), row("nn").indirect(T.lp[:, 20:40]), two("nn") + keys, ["rr"])
    def ahead_rp(): act(T.r3[:, 1:960:3], row("rr").indirect(T.lp[:, 0:20]), ["rr", "pe"], ["r3b"])
    def ahead_copy(i): gcopy(T.r3[:, 2 * i:960:3], row("rr"), C, ["rr"], ["r3" + "ac"[i]])

    def terms_u(u, f0, f3, r):
        for i, f in ((0, f0), (3, f3)): emit("s", lambda e: e.activation(T.xb[:, i:100:5], u, CP, scale=col(f)), r + [f], ["xb%d" % i])

    def term_v(i, v, r):
        if i == 1: tsc(T.xb[:, 1:100:5], v, col("sq"), -1.0, [A.mult, A.mult], r + ["sq"], ["xb1"])
        else: tsc(T.xb[:, 4:100:5], v, col("we"), None, [A.mult], r + ["we"], ["xb4"])

    def unpackers(bs):
        for b in bs: quant(T["eq%d" % b][:], T["es%d" % b][:], T.et[:, 3 - b:515 - b], ["et"], ["eq%d" % b])

    def fmm(bs):
        for b in bs: mm(b, C, T["eq%d" % b][:], T["es%d" % b][:], T.tq[:], T.ts[:], ["eq%d" % b, "tq0", "tq1"])

    def fcopy(bs):
        for b in bs:
            act(run("fw", b), bank(b, C), ["ps%d" % b], ["fw%d" % b], 2.0 if b > 1 else 1.0)
            if b > 1: dma("y", run("f2", b - 2), run("fw", b), ["fw%d" % b], ["f2%d" % b])

    def mean(b, h):
        out, n, w = T.zt[:, 640 * h + b:640 * h + 640:4], nL(10 * h, 10 * h + 10), ["zt%d.%d" % (h, b)]
        if b > 1: act(out, run("yw", b - 2).indirect(n), ["yw%d" % b, "nL"], w, 0.5)
        else: tt(out, run("gw", b).indirect(n), run("g2", b, HF * h, HF * h + HF), A.add, ["gw%d" % b, "g2%d.%d" % (b, h), "nL"], w)

    def layer(h):
        c = slice(HF * h, HF * h + HF)
        quant(T.zq[:, c], T.zs[:, c], T.zt[:, 640 * h:640 * h + 640], ["zt%d.%d" % (h, b) for b in range(4)], ["zq%d" % h])
        for b in range(4):
            mm(4 * h + b, HF, T.wq[:, 128 * b:128 * b + 128], T.wsp[:, 128 * b:128 * b + 128], T.zq[:, c], T.zs[:, c], ["wq", "wsp", "zq%d" % h])

    def htile(on, tile, b0, bs):
        for b in bs:
            out, r, w = T[tile][:, b:640:4], ["ps%d" % (b0 + b)], ["%s.%d" % (tile, b)]
            if on == "s": act(out, bank(b0 + b, HF), r, w, 0.03125)
            else: tsc(out, bank(b0 + b, HF), 0.03125, None, [A.mult], r, w)

    def pack(tile, hq, hs): quant(T[hq][:], T[hs][:], T[tile][:], ["%s.%d" % (tile, b) for b in range(4)], [hq])

    def unpack(hq, hs, b0, bs):
        for b in bs: mm(b0 + b, HF, T["eq%d" % b][:], T["es%d" % b][:], T[hq][:], T[hs][:], ["eq%d" % b, hq])

    def xsum(h, b0, b): tt(run("xw", b, HF * h, HF * h + HF), run("gw", b, HF * h, HF * h + HF), bank(b0 + b, HF), A.add, ["gw%d" % b, "ps%d" % (b0 + b)], ["xw%d.%d" % (b, h)])

    def kcopy(h, b0):
        for b in (2, 3): act(run("kw", b - 2, HF * h, HF * h + HF), bank(b0 + b, HF), ["ps%d" % (b0 + b)], ["kw%d.%d" % (b, h)], 2.0)

    def invert(lo, hi): cp(run("mr", 0).indirect(nL(lo, hi)), T.w2[:, 640 + 16 * lo:640 + 16 * hi], ["idr", "nL"], ["mr"])

    def state(b, h):
        lo, hi = CUT[h]
        out, m, w = T.xst[:, 4 * lo + b:4 * hi:4], T.mL[:, lo // 16:hi // 16], ["xst%d.%d" % (h, b)]
        if b < 2: act(out, run("xw", b).indirect(m), ["xw%d.0" % b, "xw%d.1" % b, "mL"], w, 2.0)
        else: tt(out, run("kw", b - 2).indirect(m), run("fw", b, lo, hi), A.add, ["kw%d.0" % b, "kw%d.1" % b, "fw%d" % b, "mL"], w)

    def send(k, partner):
        rid, pid, _ = topo.addr(partner)
        m, n = topo.mask(core, partner), 2 * len(topo.engines(core, partner))
        order("g", "remote", ["hqp"], [])
        arr, loc = T.sem["arr%d" % k], T.sem["loc%d" % k]
        g.remote_dma(T["lq%d" % k][:].bitcast(dt.uint8), T.hqp[:].bitcast(dt.uint8), arr, loc, pid, rid, m)
        g.remote_dma(T["ls%d" % k][:], T.hsp[:], arr, loc, pid, rid, m)
        note(("remote", "loc%d" % k, n, {}), ["hqp"], [])
        note(("remote", "arr%d" % k, n, {}), [], ["lq%d" % k])
        moved.append((k, n))

    def cross(name, at, src, up, r, w):
        for a in range(4):
            lo, hi = slice(32 * a, 32 * a + 16), slice(32 * a + 16, 32 * a + 32)
            dma("y", T[name][lo if up else hi, at:at + 20], T[src][hi if up else lo, 0:20], r, ["%s%d" % (w, a)])

    def product(i, h):
        lo, hi = CUT[h]
        mm(4 + 2 * i + h, hi - lo, T.uu[:, 128 * i:128 * i + 128], T.uus[:, 128 * i:128 * i + 128], T.tq[:, lo:hi], T.ts[:, lo:hi], ["uu%d" % i, "uus%d" % i, "tq%d" % h])

    def signs(on, name, h):
        lo, hi = CUT[h]
        b = 4 + 2 * (name == "sf") + h
        if on == "v": tsc(T[name][:, lo:hi], bank(b, hi - lo), 0.0, 0.5, [A.is_gt, A.subtract], ["ps%d" % b], [name + "%d" % h])
        else: emit("s", lambda e: e.activation(T[name][:, lo:hi], bank(b, hi - lo), SG, bias=-(2.0 ** -93)), ["ps%d" % b], [name + "%d" % h])

    def agree(h):
        lo, hi = CUT[h]
        tt(T.c3[:, 3 * lo + 2:3 * hi:3], row("sa").indirect(T.lp[:, lo // 16:hi // 16]), T.sb_[:, lo:hi], A.is_equal, two("sa") + ["sb_%d" % h, "pe"], ["c3c%d" % h])

    def choose(h):
        c = slice(3 * CUT[h][0], 3 * CUT[h][1])
        scan(T.fo[:, c], T.c3[:, c], T.r3[:, c], ["c3a", "c3b", "c3c%d" % h, "r3a", "r3b", "r3c"], ["fo%d" % h])
    FO = two("fo")

    def own_signs(h):
        lo, hi = CUT[h]
        scan(T.q5[:, 5 * lo:5 * hi:5], T.dv[:, lo:hi], T.sf[:, lo:hi], DV + ["sf%d" % h], ["q5c%d" % h])

    def pair_signs(): scan(T.q5[:, 16:1616:5], row("dv"), row("spf"), DV + ["spf"], ["q5d"])
    def choice(): scan(T.qo[:], T.q5[:, 43:1632:16], T.xb[:], ["xb%d" % i for i in range(5)] + ["q5a", "q5b", "q5c0", "q5c1", "q5d", "q5e"], ["qo"])

    def onward(i, f, base):
        for a in range(4):
            c = 32 * ((a + 1) % 4)
            tsc(T.sh[c:c + 16, 20 * i:20 * i + 20], T.tb[32 * a:32 * a + 16, 16 * i:640:32], f, base, [A.mult, A.add], two("tb") + ["sh+"], ["sh%d.%d" % (i, a)])

    moved = []
    for i, h in ((0, 0), (0, 1), (1, 0), (1, 1)): product(i, h)
    ahead_r(["l1"])
    for name, h in (("sa", 0), ("sa", 1), ("sb_", 0), ("sb_", 1)): signs("s", name, h)
    ahead_copy(0)
    gg(lambda e: e.iota(T.aj[:], [[0, 2], [16, 2], [32, 10]], C, 0), [], ["aj"])
    count(run("mr", 1), [[0, C]], 0, ["mr2"])
    count(T.mG[:], [[0, 20]], 0, ["mG"])
    ahead_rp()
    tsc(col("sq"), col("inv"), col("inv"), col("mod"), [A.mult, A.mult], ["inv", "mod"], ["sq"])
    term_v(4, al, ["lb2"])
    unpackers((2, 3))
    term_v(1, al, ["lb2"])
    signs("v", "sf", 0)
    cp(T.r3[:, 2:960:3], row("rr"), ["rr"], ["r3c"])
    signs("v", "sf", 1)
    for h in (0, 1): own_signs(h)
    for k in range(ROUNDS):
        last = k == ROUNDS - 1
        partner = T.cores[rank ^ STEP[k]]
        act(row("spf"), row("sf").indirect(T.nf[:, 20:40]), two("sf") + ["pf"], ["spf"])
        for h in (0, 1): agree(h)
        if k:
            fmm((2, 3, 0, 1))
            terms_u(ends("su"), "ua", "ub", ["su"])
            fcopy((2, 3))
            pair_signs()
            choose(0)
            choice()
            choose(1)
        else:
            fmm((2, 3))
            terms_u(T.bl[:, 60:80], "sq", "wd", ["bl"])
            for h in (0, 1): choose(h)
            part("s", "b2", 0, row("fo"), "me3", 0, 4, 20, FO + ["me3"], "b21")
            fcopy((2,))
            pair_signs()
            part("v", "b2", 0, row("fo"), "me3", 0, 0, 4, FO + ["me3"], "b20")
            choice()
            unpackers((0,))
        for i in (0, 1):
            tsc(T.l3[:, i:20:2], T.qo[:, 4 + 50 * i:50 + 50 * i:5], 3.0 if k else 1.0, 482.25 if k else 0.25, [A.mult, A.add], ["qo"], ["l3%d" % i])
        if k:
            split("w2", C, row("fo"), "l3", 0, FO + two("l3"), "nm")
            fcopy((0, 1))
        else:
            unpackers((1,))
            split("w2", C, row("b2"), "l3", 0, two("b2") + two("l3"), "nm")
            tsc(T.sh[:], T.aj[:], col("pm"), None, [A.add], ["aj", "pm"], ["sh+"])
            fmm((0, 1))
            fcopy((3, 0))
        for i in (0, 1): turn(T.tb[:, C * i:C * i + C], T.w2[:, C + 16 * i:640 + 16 * i], two("nm") + ["idr"], ["tb%d" % i])
        if k == 0: tsc(T.l4[:], T.nf[:, 20:40], 320.0, None, [A.add], ["pf"], ["l4"])
        onward(1, 3.0, 482.0)
        part("s", "w2", 0, row("fo"), "sh", 20, 8, 20, FO + four("sh1."), "rw1")
        onward(0, 1.0, 160.0)
        part("v", "w2", 0, row("fo"), "sh", 20, 0, 8, FO + four("sh1."), "rw0")
        split("nn", 0, T.w2[:, 0:640], "sh", 0, two("rw") + two("nm") + four("sh0."), "nn")
        if k == 0:
            fcopy((1,))
            for f, w in (("ua", "sq"), ("ub", "wd")): tsc(col(f), col("inv"), col(w), None, [A.mult], ["inv", w], [f])
        pick("sn", "nn", two("nn"))
        if k == 0: quant(T.vq[:], T.vs[:], T.vt[:], ["vt"], ["vq"])
        tolist(nL(), "sn", "nL")
        if not last: cross("lp", 20, "nf", False, ["nL", "l1"], "l1")
        else:
            affine(row("nlf"), row("nn"), 1.0, 160.0, two("nn"), ["nlf"])
            dma("y", T.nl[:], T.nlf[0:128:16, :], ["nlf"], [])
        for b in (0, 1): act(run("gw", b), run("fw", b).indirect(nL()), ["fw%d" % b, "nL"], ["gw%d" % b])
        for b in (2, 3): tt(run("yw", b - 2), run("fw", b).indirect(nL()), run("f2", b - 2), A.add, ["fw%d" % b, "f2%d" % b, "nL"], ["yw%d" % b])
        for b in (0, 1): gcopy(run("g2", b, 0, HF), run("gw", b, 0, HF), HF, ["gw%d" % b], ["g2%d.0" % b])
        for b in (0, 1): cp(run("g2", b, HF), run("gw", b, HF), ["gw%d" % b], ["g2%d.1" % b])
        for b, h in ((2, 1), (3, 1), (2, 0), (3, 0), (0, 1), (1, 1), (0, 0)): mean(b, h)
        layer(1)
        mean(1, 0)
        layer(0)
        if not last: ahead_r(four("l1"))
        htile("s", "hp", 4, (0, 1, 3))
        htile("v", "hp", 4, (2,))
        invert(0, 4)
        pack("hp", "hqp", "hsp")
        send(k, partner)
        htile("s", "ho", 0, (0, 2, 3))
        htile("v", "ho", 0, (1,))
        invert(4, 10)
        pack("ho", "hqo", "hso")
        unpack("hqo", "hso", 4, (0, 2, 1, 3))
        invert(10, 20)
        if not last:
            for i in (0, 1): ahead_copy(i)
            ahead_rp()
            dma("y", T.mr[16:128, C:640], T.mr[0:112, 0:C], ["mr"], ["mr2"])
        unpack("lq%d" % k, "ls%d" % k, 0, (2, 0, 1, 3))
        kcopy(0, 4)
        xsum(0, 4, 0)
        pick("sm", "mr", ["mr"])
        xsum(0, 4, 1)
        tolist(row("mL"), "sm", "mL")
        if not last:
            cross("l4", 0, "mL", True, ["mL", "l4"], "l4")
            tsc(T.mF[:], ends("sm"), col("inv"), None, [A.mult], ["sm", "inv"], ["mF"])
            dma("y", T.mG[16:128, :], T.mF[0:112, :], ["mF"], ["mG"])
        kcopy(1, 0)
        for b in (0, 1): xsum(1, 0, b)
        for b, h in ((2, 0), (2, 1), (3, 0), (3, 1), (0, 0), (1, 0), (1, 1), (0, 1)): state(b, h)
        if not last: act(row("ur"), row("mr").indirect(T.l4[:]), ["mr", "mr2"] + four("l4"), ["ur"])
        for h in (0, 1): tquant("xst", h, ["xst%d.%d" % (h, b) for b in range(4)])
        if not last:
            for i, h in ((0, 0), (1, 0), (1, 1), (0, 1)): product(i, h)
            for i in (1, 4): term_v(i, T.mG[:], ["mG"])
            for h in (0, 1): signs("v", "sf", h)
            for name, h in (("sa", 0), ("sb_", 0), ("sa", 1), ("sb_", 1)): signs("s", name, h)
            pick("su", "ur", ["ur"])
            for h in (0, 1): own_signs(h)

    for h in (0, 1):
        lo, hi = CUT[h]
        mm(6 + h, hi - lo, T.vq[:], T.vs[:], T.tq[:, lo:hi], T.ts[:, lo:hi], ["vq", "tq%d" % h])
        dma("y", T.oc[:, 4 * lo:4 * hi], T.tq[:, lo:hi].bitcast(dt.uint8), ["tq%d" % h], [])
    act(T.yo[:, 0:T0], bank(6, T0), ["ps6"], ["yo0"])
    cp(T.yo[:, T0:C], bank(7, C - T0), ["ps7"], ["yo1"])
    dma("s", T.y[:, 0:T0], T.yo[:, 0:T0], ["yo0"], [])
    for i in range(4): dma("y" if i < 2 else "s", T.osc[4 * i:4 * i + 4, :], T.ts[32 * i:32 * i + 4, :], ["tq0", "tq1"], [])
    dma("y", T.y[:, T0:C], T.yo[:, T0:C], ["yo1"], [])
    for k, n in moved:
        need("g", ("x", "loc%d" % k, n, {}))
    for q, s in semof.items(): need("g", ("x", s, cnt[s], known[q]))
    for i in range(ndma[0]):
        if not any(known[q].get("dm%d" % i) for q in queue): need("g", ("x", "dm%d" % i, 16, {}))
